import numpy as np
import ml_dtypes


def mxq(x, axis, fmt="e4m3"):
    dtype, down = {"e4m3": (ml_dtypes.float8_e4m3fn, 7), "e5m2": (ml_dtypes.float8_e5m2, 14)}[fmt]
    v = np.moveaxis(np.asarray(x, np.float32).astype(ml_dtypes.bfloat16).astype(np.float64), axis, -1)
    blocks = v.reshape(v.shape[:-1] + (-1, 32))
    amax = np.abs(blocks).max(-1, keepdims=True)
    byte = np.maximum(np.where(amax > 0, np.frexp(amax)[1] - 1 + 127, 0) - down, 1)
    scale = np.exp2(byte - 127.0)
    codes = (blocks / scale).astype(np.float32).astype(dtype).astype(np.float64)
    return np.moveaxis((codes * scale).reshape(v.shape), -1, axis)


WIDE = False


def mx_kscale(k):
    if not WIDE:
        return np.ones(k)
    levels = np.array([24, -24, 12, -12, 0])
    if k % 512:
        return np.exp2(np.random.permutation(np.resize(levels, k // 32))).repeat(32)
    a = np.empty((k // 512, 16))
    for p in range(k // 512):
        a[p, :8] = np.random.permutation(np.resize(levels, 8))
        for g in range(8):
            far = levels[np.abs(levels - a[p, g]) >= 10]
            a[p, g + 8] = far[np.random.randint(len(far))]
    return np.exp2(a.ravel()).repeat(32)


def f64(x):
    return np.asarray(x).astype(np.float64)


def striped8(idx):
    return np.concatenate([v.reshape(-1, 16).T for v in idx]).astype(np.uint16)


def unstriped8(offs):
    return np.stack([offs[16 * g:16 * g + 16].T.reshape(-1) for g in range(8)]).astype(np.int64)


E2M1 = np.array([0.0, 0.5, 1.0, 1.5, 2.0, 3.0, 4.0, 6.0, -0.0, -0.5, -1.0, -1.5, -2.0, -3.0, -4.0, -6.0])


def pack_weight(w, fmt):
    k, n = w.shape
    w = f64(np.asarray(w, np.float32).astype(ml_dtypes.bfloat16)).reshape(k // 32, 32, n)
    amax = np.abs(w).max(1)
    if fmt == "e4m3":
        byte = np.frexp(amax)[1] - 1 + 127 - 7
    else:
        mant, ex = np.frexp(amax / 6.0)
        byte = np.where(mant > 0.5, ex, ex - 1) + 127
    byte = np.clip(np.where(amax > 0, byte, 1), 1, 254)
    scaled = (w * np.exp2(127.0 - byte)[:, None, :]).reshape(k, n).astype(np.float32)
    by_word = np.ascontiguousarray(scaled.reshape(k // 512, 128, 4, n).transpose(0, 1, 3, 2))
    if fmt == "e4m3":
        words = by_word.astype(ml_dtypes.float8_e4m3fn).view(np.uint8)
    else:
        c = by_word.astype(ml_dtypes.float4_e2m1fn).view(np.uint8) & 0xF
        words = (c[..., 0::2] | (c[..., 1::2] << 4)).reshape(k // 512, 128, 2 * n)
    return np.ascontiguousarray(words), np.ascontiguousarray(byte.astype(np.uint8).reshape(k // 512, 16, n))


def unpack_weight(words, scales, fmt):
    g, _, n = scales.shape
    words = np.ascontiguousarray(words).reshape(g, 128, n, -1)
    if fmt == "e4m3":
        vals = words.view(ml_dtypes.float8_e4m3fn).astype(np.float64)
    else:
        nib = np.empty((g, 128, n, 4), np.uint8)
        nib[..., 0::2] = words & 0xF
        nib[..., 1::2] = words >> 4
        vals = E2M1[nib]
    vals = vals * np.repeat(np.exp2(scales.astype(np.float64) - 127.0), 8, axis=1)[..., None]
    return vals.transpose(0, 1, 3, 2).reshape(g * 512, n)


def planes(y):
    n, m = y.shape
    v = y.astype(np.float32).astype(ml_dtypes.bfloat16).astype(np.float64).reshape(n // 32, 32, m)
    top = np.abs(v).max(1)
    byte = np.clip(np.where(top > 0, np.frexp(top)[1] - 1 + 127 - 7, 1), 1, 254)
    codes = (v * np.exp2(127.0 - byte)[:, None, :]).reshape(n, m).astype(np.float32).astype(ml_dtypes.float8_e4m3fn).view(np.uint8)
    words = codes.reshape(n // 512, 128, 4, m).transpose(0, 1, 3, 2)
    return np.ascontiguousarray(words), np.ascontiguousarray(byte.astype(np.uint8).reshape(n // 512, 16, m))


K, L, N, T, J = 1024, 512, 512, 2048, 1024


def setup_inputs():
    n = np.random.standard_normal
    s = mx_kscale(K)[:, None]
    s2 = mx_kscale(L)[:, None]
    p_wt = pack_weight(n((K, N)) / np.sqrt(K) / s, "e4m3")
    p_wx = pack_weight(n((L, N)) / np.sqrt(L) / s2, "e2m1")
    return {
        "xT": (n((K, T)) * s).astype(np.float32),
        "wgt": np.repeat(np.random.uniform(0.5, 2.0, (8, J)), 16, axis=0).astype(np.float32),
        "wt_words": p_wt[0],
        "wt_scales": p_wt[1],
        "c": (n((L, J)) * s2).astype(np.float32),
        "wx_words": p_wx[0],
        "wx_scales": p_wx[1],
        "offs": striped8(np.stack([np.random.permutation(T)[:J] for _ in range(8)])),
    }


def reference(xT, wgt, wt_words, wt_scales, c, wx_words, wx_scales, offs):
    idx = unstriped8(offs)
    rows = np.arange(K)
    xg = f64(wgt)[rows // 4 % 128] * f64(xT)[rows[:, None], idx[rows % 512 // 64]]
    xT_ = mxq(xg, 0, "e4m3")
    wt_ = unpack_weight(wt_words, wt_scales, "e4m3")
    c_q_ = mxq(f64(c), 0, "e4m3")
    c_r_ = mxq(f64(c) - c_q_, 0, "e4m3")
    wx_ = unpack_weight(wx_words, wx_scales, "e2m1")
    y = wt_.T @ xT_ + wx_.T @ c_q_ + wx_.T @ c_r_
    return (y,) + planes(y)

@@ -1,0 +1,225 @@
+from contextlib import ExitStack
+
+import concourse.mybir as mybir
+
+K, L, N, T, J = 1024, 512, 512, 2048, 1024
+FLOPS = 2 * N * J * (K + 3 * L)
+
+F32 = mybir.dt.float32
+BF16 = mybir.dt.bfloat16
+I32 = mybir.dt.int32
+U32 = mybir.dt.uint32
+U16 = mybir.dt.uint16
+U8 = mybir.dt.uint8
+FP8X4 = mybir.dt.float8_e4m3fn_x4
+FP4X4 = mybir.dt.float4_e2m1fn_x4
+MULT = mybir.AluOpType.mult
+SUB = mybir.AluOpType.subtract
+
+P = 128
+PACK = 4
+BANK_COLS = 128
+CHUNK = 256
+HALF = 512
+
+
+def woven(ap):
+    return ap.rearrange("p (c i t) -> p c t i", i=4, t=PACK)
+
+
+def by_rows(ap):
+    return ap.rearrange("p t (c i) -> p c t i", i=4)
+
+
+def tile_list_noneP_kernel(
+    tc, xT, wgt, wt_words, wt_scales, c, wx_words, wx_scales, offs, out_0, out_1, out_2
+):
+    nc = tc.nc
+    with ExitStack() as ctx:
+        keep = ctx.enter_context(tc.tile_pool(name="keep", bufs=1))
+        ring = ctx.enter_context(tc.tile_pool(name="ring", bufs=2))
+        back_psum = ctx.enter_context(tc.psum_pool(name="back_psum", bufs=2))
+        y_psum = ctx.enter_context(tc.psum_pool(name="y_psum", bufs=6))
+
+        offsets = keep.tile([P, J // 16], U16, name="offsets")
+        nc.sync.dma_start(offsets[:], offs)
+
+        wx_raw = keep.tile([P, 2 * N], U8, name="wx_raw", align_bytes=64)
+        nc.sync.dma_start(wx_raw[:].bitcast(I32), wx_words[0].bitcast(I32))
+        wt_raw = keep.tile([P, 2, N], I32, name="wt_raw", align_bytes=64)
+        nc.sync.dma_start(wt_raw[:], wt_words.rearrange("a p n i -> p a (n i)").bitcast(I32))
+
+        scales_raw = keep.tile([P, N], U8, name="scales_raw", align_bytes=64)
+        nc.gpsimd.memset(scales_raw[:].bitcast(I32), 0)
+        eye = keep.tile([P, PACK * P * PACK], BF16, name="eye", align_bytes=64)
+        nc.gpsimd.memset(eye[:], 0.0)
+        eye_view = eye[:].rearrange("p (t m i) -> p t m i", t=PACK, i=PACK)
+        nc.gpsimd.affine_select(
+            out=eye_view,
+            in_=eye_view,
+            compare_op=mybir.AluOpType.not_equal,
+            fill=1.0,
+            base=0,
+            pattern=[[P, PACK], [-1, P], [-P, PACK]],
+            channel_multiplier=1,
+        )
+        for q in range(4):
+            nc.gpsimd.dma_start(
+                scales_raw[32 * q : 32 * q + 4, :].bitcast(I32), wx_scales[0, 4 * q : 4 * q + 4, :].bitcast(I32)
+            )
+            nc.gpsimd.dma_start(
+                scales_raw[32 * q + 4 : 32 * q + 12, :].bitcast(I32), wt_scales[:, 4 * q : 4 * q + 4, :].bitcast(I32)
+            )
+
+        w_sb = keep.tile([P, J], F32, name="w_sb")
+        planes = [keep.tile([P, T], F32, name="plane%d" % u) for u in range(8)]
+        c_sb = [keep.tile([P, PACK, CHUNK], F32, name="c%d" % k) for k in range(J // CHUNK)]
+        x_rows = xT.rearrange("(a p i) t -> a i p t", a=2, i=PACK)
+        c_rows = c.rearrange("(p t) j -> p t j", t=PACK)
+
+        def load_plane(u):
+            nc.sync.dma_start(planes[u][:], x_rows[u // PACK, u % PACK])
+
+        def load_c(k):
+            nc.sync.dma_start(c_sb[k][:], c_rows[:, :, k * CHUNK : (k + 1) * CHUNK])
+
+        nc.sync.dma_start(w_sb[:, 0:HALF], wgt[:, 0:HALF])
+        load_plane(0)
+        load_c(0)
+        load_plane(1)
+        load_plane(2)
+        load_c(1)
+        load_plane(3)
+        nc.sync.dma_start(w_sb[:, HALF:J], wgt[:, HALF:J])
+        for u in range(4, 8):
+            load_plane(u)
+        load_c(2)
+        load_c(3)
+
+        wx_dealt = keep.tile([P, 2 * N], U8, name="wx_dealt", align_bytes=64)
+        nc.vector.tensor_copy(
+            wx_dealt[:].rearrange("p (t g m b) -> p g t m b", t=PACK, m=8, b=2),
+            wx_raw[:].rearrange("p (g m t b) -> p g t m b", t=PACK, m=8, b=2),
+        )
+        wt_dealt = keep.tile([P, 2, N], I32, name="wt_dealt", align_bytes=64)
+        nc.vector.tensor_copy(
+            wt_dealt[:].rearrange("p a (t g m) -> p a g t m", t=PACK, m=4),
+            wt_raw[:].rearrange("p a (g m t) -> p a g t m", t=PACK, m=4),
+        )
+        eye_codes = keep.tile([P, PACK * P], U32, name="eye_codes", align_bytes=64)
+        eye_scales = keep.tile([P, PACK * P], U8, name="eye_scales", align_bytes=64)
+        nc.vector.quantize_mx(out=eye_codes[:].bitcast(FP8X4), scales=eye_scales[:], in_=eye[:])
+        scales_dealt = keep.tile([P, N], U8, name="scales_dealt", align_bytes=64)
+        nc.vector.tensor_copy(
+            scales_dealt[:].rearrange("p (t g m) -> p g t m", t=PACK, m=16),
+            scales_raw[:].rearrange("p (g m t) -> p g t m", t=PACK, m=16),
+        )
+
+        xq = {}
+        cq = {}
+        cr = {}
+
+        def quantised(name, src, width):
+            codes = keep.tile([P, width], U32, name=name + "_codes", align_bytes=64)
+            scales = keep.tile([P, width], U8, name=name + "_scales", align_bytes=64)
+            nc.vector.quantize_mx(out=codes[:].bitcast(FP8X4), scales=scales[:], in_=src)
+            return codes, scales
+
+        def pick(a, j0, width):
+            picked = ring.tile([P, PACK, width], F32, name="picked", tag="picked")
+            for i in range(PACK):
+                nc.vector.tensor_tensor(
+                    picked[:, i, :],
+                    planes[PACK * a + i][:].indirect(offsets[:, j0 // 16 : (j0 + width) // 16]),
+                    w_sb[:, j0 : j0 + width],
+                    MULT,
+                )
+            rounded = keep.tile([P, PACK * width], BF16, name="xg%d_%d" % (a, j0), align_bytes=64)
+            nc.scalar.copy(woven(rounded[:]), by_rows(picked[:]))
+            codes, scales = quantised("xq%d_%d" % (a, j0), rounded[:], width)
+            for s in range(0, width, BANK_COLS):
+                xq[(a, j0 + s)] = (codes[:, s : s + BANK_COLS], scales[:, s : s + BANK_COLS])
+
+        def tiers(k):
+            rounded = keep.tile([P, PACK * CHUNK], BF16, name="cb%d" % k, align_bytes=64)
+            nc.scalar.copy(woven(rounded[:]), by_rows(c_sb[k][:]))
+            codes, scales = quantised("cq%d" % k, rounded[:], CHUNK)
+            left = keep.tile([P, PACK * CHUNK], BF16, name="left%d" % k, align_bytes=64)
+            for s in range(0, CHUNK, BANK_COLS):
+                cq[k * CHUNK + s] = (codes[:, s : s + BANK_COLS], scales[:, s : s + BANK_COLS])
+                back = back_psum.tile([P, PACK, BANK_COLS], F32, name="back")
+                for t in range(PACK):
+                    nc.tensor.matmul_mx(
+                        out=back[:, t, :],
+                        lhsT=eye_codes[:, t * P : (t + 1) * P].bitcast(FP8X4),
+                        lhsT_scale=eye_scales[:, t * P : (t + 1) * P],
+                        rhs=codes[:, s : s + BANK_COLS].bitcast(FP8X4),
+                        rhs_scale=scales[:, s : s + BANK_COLS],
+                        start=True,
+                        stop=True,
+                    )
+                nc.vector.tensor_tensor(
+                    woven(left[:, PACK * s : PACK * (s + BANK_COLS)]),
+                    by_rows(c_sb[k][:, :, s : s + BANK_COLS]),
+                    by_rows(back[:]),
+                    SUB,
+                )
+            codes, scales = quantised("cr%d" % k, left[:], CHUNK)
+            for s in range(0, CHUNK, BANK_COLS):
+                cr[k * CHUNK + s] = (codes[:, s : s + BANK_COLS], scales[:, s : s + BANK_COLS])
+
+        y_codes = keep.tile([P, J], U32, name="y_codes", align_bytes=64)
+        y_scales = keep.tile([P, J], U8, name="y_scales", align_bytes=64)
+        y_rows = out_0.rearrange("(p t) j -> p t j", t=PACK)
+        words_out = out_1[0].rearrange("p j i -> p (j i)").bitcast(I32)
+
+        def project(j0, width):
+            y_sb = keep.tile([P, PACK, width], F32, name="y%d" % j0)
+            rounded = keep.tile([P, PACK * width], BF16, name="yb%d" % j0, align_bytes=64)
+            for s in range(0, width, BANK_COLS):
+                acc = y_psum.tile([P, PACK, BANK_COLS], F32, name="acc")
+                j = j0 + s
+                for step, (codes, scales) in enumerate((cq[j], cr[j], xq[(0, j)], xq[(1, j)])):
+                    for t in range(PACK):
+                        cols = slice(t * P, (t + 1) * P)
+                        if step < 2:
+                            lhs = wx_dealt[:, 2 * t * P : 2 * (t + 1) * P].bitcast(FP4X4)
+                            lhs_scale = scales_dealt[:, cols]
+                        else:
+                            lhs = wt_dealt[:, step - 2, cols].bitcast(FP8X4)
+                            lhs_scale = scales_dealt[4 * (step - 1) : P, cols]
+                        nc.tensor.matmul_mx(
+                            out=acc[:, t, :],
+                            lhsT=lhs,
+                            lhsT_scale=lhs_scale,
+                            rhs=codes.bitcast(FP8X4),
+                            rhs_scale=scales,
+                            start=(step == 0 and t == 0),
+                            stop=(step == 3 and t == PACK - 1),
+                        )
+                nc.scalar.copy(woven(rounded[:, PACK * s : PACK * (s + BANK_COLS)]), by_rows(acc[:]))
+                nc.scalar.copy(y_sb[:, :, s : s + BANK_COLS], acc[:])
+            cols = slice(j0, j0 + width)
+            nc.vector.quantize_mx(out=y_codes[:, cols].bitcast(FP8X4), scales=y_scales[:, cols], in_=rounded[:])
+            nc.sync.dma_start(y_rows[:, :, cols], y_sb[:])
+            nc.sync.dma_start(words_out[:, cols], y_codes[:, cols].bitcast(I32))
+
+        pick(0, 0, HALF)
+        tiers(0)
+        tiers(1)
+        pick(1, 0, HALF)
+        project(0, CHUNK)
+        project(CHUNK, CHUNK)
+        pick(0, HALF, HALF)
+        tiers(2)
+        tiers(3)
+        pick(1, 512, 256)
+        project(512, 256)
+        pick(1, 768, 128)
+        project(768, 128)
+        pick(1, 896, 128)
+        project(896, 128)
+        for q in range(4):
+            nc.scalar.dma_start(
+                out_2[0, 4 * q : 4 * q + 4, :].bitcast(I32), y_scales[32 * q : 32 * q + 4, :].bitcast(I32)
+            )

@@ -1,6 +1,7 @@
 from contextlib import ExitStack
 
 import concourse.mybir as mybir
+from concourse.masks import make_identity
 
 K, L, N, T, J = 1024, 512, 512, 2048, 1024
 FLOPS = 2 * N * J * (K + 3 * L)
@@ -37,7 +38,7 @@ def tile_list_noneP_kernel(
     nc = tc.nc
     with ExitStack() as ctx:
         keep = ctx.enter_context(tc.tile_pool(name="keep", bufs=1))
-        ring = ctx.enter_context(tc.tile_pool(name="ring", bufs=2))
+        ring = ctx.enter_context(tc.tile_pool(name="ring", bufs=1))
         back_psum = ctx.enter_context(tc.psum_pool(name="back_psum", bufs=2))
         y_psum = ctx.enter_context(tc.psum_pool(name="y_psum", bufs=6))
 
@@ -50,29 +51,24 @@ def tile_list_noneP_kernel(
         nc.sync.dma_start(wt_raw[:], wt_words.rearrange("a p n i -> p a (n i)").bitcast(I32))
 
         scales_raw = keep.tile([P, N], U8, name="scales_raw", align_bytes=64)
-        nc.gpsimd.memset(scales_raw[:].bitcast(I32), 0)
+        nc.vector.memset(scales_raw[:].bitcast(I32), 0)
+        square = keep.tile([P, P], BF16, name="square")
+        make_identity(nc, square[:])
         eye = keep.tile([P, PACK * P * PACK], BF16, name="eye", align_bytes=64)
-        nc.gpsimd.memset(eye[:], 0.0)
-        eye_view = eye[:].rearrange("p (t m i) -> p t m i", t=PACK, i=PACK)
-        nc.gpsimd.affine_select(
-            out=eye_view,
-            in_=eye_view,
-            compare_op=mybir.AluOpType.not_equal,
-            fill=1.0,
-            base=0,
-            pattern=[[P, PACK], [-1, P], [-P, PACK]],
-            channel_multiplier=1,
-        )
-        for q in range(4):
-            nc.gpsimd.dma_start(
+        nc.vector.memset(eye[:], 0.0)
+        for t in range(PACK):
+            nc.vector.tensor_copy(eye[:, PACK * P * t + t : PACK * P * (t + 1) : PACK], square[:])
+
+        def load_scales(q):
+            nc.sync.dma_start(
                 scales_raw[32 * q : 32 * q + 4, :].bitcast(I32), wx_scales[0, 4 * q : 4 * q + 4, :].bitcast(I32)
             )
-            nc.gpsimd.dma_start(
+            nc.sync.dma_start(
                 scales_raw[32 * q + 4 : 32 * q + 12, :].bitcast(I32), wt_scales[:, 4 * q : 4 * q + 4, :].bitcast(I32)
             )
 
         w_sb = keep.tile([P, J], F32, name="w_sb")
-        planes = [keep.tile([P, T], F32, name="plane%d" % u) for u in range(8)]
+        planes = [keep.tile([P, T], F32, name="plane%d" % u, align_bytes=64) for u in range(8)]
         c_sb = [keep.tile([P, PACK, CHUNK], F32, name="c%d" % k) for k in range(J // CHUNK)]
         x_rows = xT.rearrange("(a p i) t -> a i p t", a=2, i=PACK)
         c_rows = c.rearrange("(p t) j -> p t j", t=PACK)
@@ -83,18 +79,23 @@ def tile_list_noneP_kernel(
         def load_c(k):
             nc.sync.dma_start(c_sb[k][:], c_rows[:, :, k * CHUNK : (k + 1) * CHUNK])
 
-        nc.sync.dma_start(w_sb[:, 0:HALF], wgt[:, 0:HALF])
+        nc.sync.dma_start(w_sb[:], wgt)
         load_plane(0)
         load_c(0)
         load_plane(1)
         load_plane(2)
+        load_scales(0)
         load_c(1)
+        load_scales(1)
         load_plane(3)
-        nc.sync.dma_start(w_sb[:, HALF:J], wgt[:, HALF:J])
-        for u in range(4, 8):
-            load_plane(u)
+        load_scales(2)
+        load_plane(4)
+        load_scales(3)
+        load_plane(5)
         load_c(2)
+        load_plane(6)
         load_c(3)
+        load_plane(7)
 
         wx_dealt = keep.tile([P, 2 * N], U8, name="wx_dealt", align_bytes=64)
         nc.vector.tensor_copy(
@@ -119,14 +120,14 @@ def tile_list_noneP_kernel(
         cq = {}
         cr = {}
 
-        def quantised(name, src, width):
-            codes = keep.tile([P, width], U32, name=name + "_codes", align_bytes=64)
+        def quantised(name, src, width, slot=None):
+            codes = keep.tile([P, width], U32, name=name + "_codes", tag=slot or name, align_bytes=64)
             scales = keep.tile([P, width], U8, name=name + "_scales", align_bytes=64)
             nc.vector.quantize_mx(out=codes[:].bitcast(FP8X4), scales=scales[:], in_=src)
             return codes, scales
 
-        def pick(a, j0, width):
-            picked = ring.tile([P, PACK, width], F32, name="picked", tag="picked")
+        def pick(a, j0, width, slot):
+            picked = ring.tile([P, PACK, width], F32, name="picked", tag=slot)
             for i in range(PACK):
                 nc.vector.tensor_tensor(
                     picked[:, i, :],
@@ -134,17 +135,20 @@ def tile_list_noneP_kernel(
                     w_sb[:, j0 : j0 + width],
                     MULT,
                 )
-            rounded = keep.tile([P, PACK * width], BF16, name="xg%d_%d" % (a, j0), align_bytes=64)
-            nc.scalar.copy(woven(rounded[:]), by_rows(picked[:]))
-            codes, scales = quantised("xq%d_%d" % (a, j0), rounded[:], width)
-            for s in range(0, width, BANK_COLS):
-                xq[(a, j0 + s)] = (codes[:, s : s + BANK_COLS], scales[:, s : s + BANK_COLS])
+            part = min(width, HALF)
+            for s0 in range(0, width, part):
+                rounded = keep.tile([P, PACK * part], BF16, name="xg", tag="xg%d_%d" % (a, j0 + s0), align_bytes=64)
+                nc.scalar.copy(woven(rounded[:]), by_rows(picked[:, :, s0 : s0 + part]))
+                codes, scales = quantised("xq%d_%d" % (a, j0 + s0), rounded[:], part)
+                for s in range(0, part, BANK_COLS):
+                    xq[(a, j0 + s0 + s)] = (codes[:, s : s + BANK_COLS], scales[:, s : s + BANK_COLS])
 
-        def tiers(k):
+        def tiers(k, parts, slot, codes_slot):
+            rows = c_sb[k][:]
             rounded = keep.tile([P, PACK * CHUNK], BF16, name="cb%d" % k, align_bytes=64)
-            nc.scalar.copy(woven(rounded[:]), by_rows(c_sb[k][:]))
-            codes, scales = quantised("cq%d" % k, rounded[:], CHUNK)
-            left = keep.tile([P, PACK * CHUNK], BF16, name="left%d" % k, align_bytes=64)
+            nc.scalar.copy(woven(rounded[:]), by_rows(rows))
+            codes, scales = quantised("cq%d" % k, rounded[:], CHUNK, codes_slot)
+            left = keep.tile([P, PACK * CHUNK], BF16, name="left%d" % k, tag=slot, align_bytes=64)
             for s in range(0, CHUNK, BANK_COLS):
                 cq[k * CHUNK + s] = (codes[:, s : s + BANK_COLS], scales[:, s : s + BANK_COLS])
                 back = back_psum.tile([P, PACK, BANK_COLS], F32, name="back")
@@ -160,26 +164,30 @@ def tile_list_noneP_kernel(
                     )
                 nc.vector.tensor_tensor(
                     woven(left[:, PACK * s : PACK * (s + BANK_COLS)]),
-                    by_rows(c_sb[k][:, :, s : s + BANK_COLS]),
+                    by_rows(rows[:, :, s : s + BANK_COLS]),
                     by_rows(back[:]),
                     SUB,
                 )
-            codes, scales = quantised("cr%d" % k, left[:], CHUNK)
-            for s in range(0, CHUNK, BANK_COLS):
-                cr[k * CHUNK + s] = (codes[:, s : s + BANK_COLS], scales[:, s : s + BANK_COLS])
+            width = CHUNK // parts
+            for s0 in range(0, CHUNK, width):
+                codes, scales = quantised("cr%d_%d" % (k, s0), left[:, PACK * s0 : PACK * (s0 + width)], width)
+                for s in range(0, width, BANK_COLS):
+                    cr[k * CHUNK + s0 + s] = (codes[:, s : s + BANK_COLS], scales[:, s : s + BANK_COLS])
 
         y_codes = keep.tile([P, J], U32, name="y_codes", align_bytes=64)
         y_scales = keep.tile([P, J], U8, name="y_scales", align_bytes=64)
         y_rows = out_0.rearrange("(p t) j -> p t j", t=PACK)
         words_out = out_1[0].rearrange("p j i -> p (j i)").bitcast(I32)
 
-        def project(j0, width):
+        def project(j0, width, order, drain):
             y_sb = keep.tile([P, PACK, width], F32, name="y%d" % j0)
             rounded = keep.tile([P, PACK * width], BF16, name="yb%d" % j0, align_bytes=64)
             for s in range(0, width, BANK_COLS):
                 acc = y_psum.tile([P, PACK, BANK_COLS], F32, name="acc")
                 j = j0 + s
-                for step, (codes, scales) in enumerate((cq[j], cr[j], xq[(0, j)], xq[(1, j)])):
+                operands = (cq[j], cr[j], xq[(0, j)], xq[(1, j)])
+                for step in order:
+                    codes, scales = operands[step]
                     for t in range(PACK):
                         cols = slice(t * P, (t + 1) * P)
                         if step < 2:
@@ -194,32 +202,32 @@ def tile_list_noneP_kernel(
                             lhsT_scale=lhs_scale,
                             rhs=codes.bitcast(FP8X4),
                             rhs_scale=scales,
-                            start=(step == 0 and t == 0),
-                            stop=(step == 3 and t == PACK - 1),
+                            start=(step == order[0] and t == 0),
+                            stop=(step == order[3] and t == PACK - 1),
                         )
                 nc.scalar.copy(woven(rounded[:, PACK * s : PACK * (s + BANK_COLS)]), by_rows(acc[:]))
-                nc.scalar.copy(y_sb[:, :, s : s + BANK_COLS], acc[:])
+                drain(y_sb[:, :, s : s + BANK_COLS], acc[:])
             cols = slice(j0, j0 + width)
             nc.vector.quantize_mx(out=y_codes[:, cols].bitcast(FP8X4), scales=y_scales[:, cols], in_=rounded[:])
             nc.sync.dma_start(y_rows[:, :, cols], y_sb[:])
             nc.sync.dma_start(words_out[:, cols], y_codes[:, cols].bitcast(I32))
 
-        pick(0, 0, HALF)
-        tiers(0)
-        tiers(1)
-        pick(1, 0, HALF)
-        project(0, CHUNK)
-        project(CHUNK, CHUNK)
-        pick(0, HALF, HALF)
-        tiers(2)
-        tiers(3)
-        pick(1, 512, 256)
-        project(512, 256)
-        pick(1, 768, 128)
-        project(768, 128)
-        pick(1, 896, 128)
-        project(896, 128)
+        pick(0, 0, J, "wide")
+        tiers(0, 1, "plane1", None)
+        tiers(1, 1, "plane3", None)
+        pick(1, 0, CHUNK, "even")
+        pick(1, CHUNK, CHUNK, "odd")
+        project(0, CHUNK, (0, 1, 2, 3), nc.scalar.copy)
+        project(CHUNK, CHUNK, (0, 1, 2, 3), nc.scalar.copy)
+        pick(1, 512, CHUNK, "even")
+        pick(1, 768, CHUNK, "odd")
+        tiers(2, 1, "left2", "xg1_0")
+        tiers(3, 2, "left3", "xg1_256")
+        project(512, 256, (2, 3, 0, 1), nc.scalar.copy)
+        project(768, 128, (2, 3, 0, 1), nc.vector.tensor_copy)
+        project(896, 128, (2, 3, 0, 1), nc.vector.tensor_copy)
         for q in range(4):
-            nc.scalar.dma_start(
+            queue = nc.scalar if q % 2 else nc.sync
+            queue.dma_start(
                 out_2[0, 4 * q : 4 * q + 4, :].bitcast(I32), y_scales[32 * q : 32 * q + 4, :].bitcast(I32)
             )

@@ -16,20 +16,31 @@ FP8X4 = mybir.dt.float8_e4m3fn_x4
 FP4X4 = mybir.dt.float4_e2m1fn_x4
 MULT = mybir.AluOpType.mult
 SUB = mybir.AluOpType.subtract
+COPY = mybir.ActivationFunctionType.Copy
 
 P = 128
 PACK = 4
-BANK_COLS = 128
+LIST_ROWS = 16
+BLOCK = 128
 CHUNK = 256
 HALF = 512
+RUN = 4
+
+VALUE_BANKS = (4, 5)
+TURN_BANKS = (6, 7)
+TURN_BACK_BANK = 3
+Y_BANKS = (0, 1, 2, 3, 6, 7, 0, 1)
+
+PICKS_LAST = (0, 1, 2, 3)
+TIERS_LAST = (2, 3, 0, 1)
 
 
 def woven(ap):
-    return ap.rearrange("p (c i t) -> p c t i", i=4, t=PACK)
+    return ap.rearrange("p (g r t) -> p g t r", r=RUN, t=PACK)
 
 
 def by_rows(ap):
-    return ap.rearrange("p t (c i) -> p c t i", i=4)
+    return ap.rearrange("p t (g r) -> p g t r", r=RUN)
 
 
 def tile_list_noneP_kernel(
@@ -38,11 +49,11 @@ def tile_list_noneP_kernel(
     nc = tc.nc
     with ExitStack() as ctx:
         keep = ctx.enter_context(tc.tile_pool(name="keep", bufs=1))
-        ring = ctx.enter_context(tc.tile_pool(name="ring", bufs=1))
-        back_psum = ctx.enter_context(tc.psum_pool(name="back_psum", bufs=2))
-        y_psum = ctx.enter_context(tc.psum_pool(name="y_psum", bufs=6))
+        gathered = ctx.enter_context(tc.tile_pool(name="gathered", bufs=1))
+        psum = ctx.enter_context(tc.psum_pool(name="psum", bufs=1))
+        stage = ctx.enter_context(tc.tile_pool(name="stage", bufs=2))
 
-        offsets = keep.tile([P, J // 16], U16, name="offsets")
+        offsets = keep.tile([P, J // LIST_ROWS], U16, name="offsets")
         nc.sync.dma_start(offsets[:], offs)
 
         wx_raw = keep.tile([P, 2 * N], U8, name="wx_raw", align_bytes=64)
@@ -52,7 +63,8 @@ def tile_list_noneP_kernel(
 
         scales_raw = keep.tile([P, N], U8, name="scales_raw", align_bytes=64)
         nc.vector.memset(scales_raw[:].bitcast(I32), 0)
-        square = keep.tile([P, P], BF16, name="square")
+
+        square = keep.tile([P, P], F32, name="square")
         make_identity(nc, square[:])
         eye = keep.tile([P, PACK * P * PACK], BF16, name="eye", align_bytes=64)
         nc.vector.memset(eye[:], 0.0)
@@ -68,33 +80,29 @@ def tile_list_noneP_kernel(
             )
 
         w_sb = keep.tile([P, J], F32, name="w_sb")
-        planes = [keep.tile([P, T], F32, name="plane%d" % u, align_bytes=64) for u in range(8)]
-        c_sb = [keep.tile([P, PACK, CHUNK], F32, name="c%d" % k) for k in range(J // CHUNK)]
-        x_rows = xT.rearrange("(a p i) t -> a i p t", a=2, i=PACK)
+        planes = [keep.tile([P, T], F32, name="plane%d" % u, align_bytes=64) for u in range(2 * PACK)]
+        c_parts = ((0, CHUNK), (CHUNK, CHUNK), (HALF, HALF))
+        c_sb = [keep.tile([P, PACK, width], F32, name="c%d" % j0) for j0, width in c_parts]
+        x_rows = xT.rearrange("(a p t) s -> a t p s", a=2, t=PACK)
         c_rows = c.rearrange("(p t) j -> p t j", t=PACK)
 
         def load_plane(u):
             nc.sync.dma_start(planes[u][:], x_rows[u // PACK, u % PACK])
 
-        def load_c(k):
-            nc.sync.dma_start(c_sb[k][:], c_rows[:, :, k * CHUNK : (k + 1) * CHUNK])
+        def load_c(part):
+            j0, width = c_parts[part]
+            nc.sync.dma_start(c_sb[part][:], c_rows[:, :, j0 : j0 + width])
 
         nc.sync.dma_start(w_sb[:], wgt)
         load_plane(0)
         load_c(0)
         load_plane(1)
-        load_plane(2)
-        load_scales(0)
         load_c(1)
-        load_scales(1)
-        load_plane(3)
-        load_scales(2)
-        load_plane(4)
-        load_scales(3)
-        load_plane(5)
+        for q in range(4):
+            load_scales(q)
+            load_plane(2 + q)
         load_c(2)
         load_plane(6)
-        load_c(3)
         load_plane(7)
 
         wx_dealt = keep.tile([P, 2 * N], U8, name="wx_dealt", align_bytes=64)
@@ -116,116 +124,172 @@ def tile_list_noneP_kernel(
             scales_raw[:].rearrange("p (g m t) -> p g t m", t=PACK, m=16),
         )
 
-        xq = {}
+        xq = ({}, {})
         cq = {}
         cr = {}
 
-        def quantised(name, src, width, slot=None):
+        def quantise(into, name, src, j0, width, slot=None):
             codes = keep.tile([P, width], U32, name=name + "_codes", tag=slot or name, align_bytes=64)
             scales = keep.tile([P, width], U8, name=name + "_scales", align_bytes=64)
             nc.vector.quantize_mx(out=codes[:].bitcast(FP8X4), scales=scales[:], in_=src)
-            return codes, scales
+            for s in range(0, width, BLOCK):
+                into[j0 + s] = (codes[:, s : s + BLOCK], scales[:, s : s + BLOCK])
 
-        def pick(a, j0, width, slot):
-            picked = ring.tile([P, PACK, width], F32, name="picked", tag=slot)
-            for i in range(PACK):
-                nc.vector.tensor_tensor(
-                    picked[:, i, :],
-                    planes[PACK * a + i][:].indirect(offsets[:, j0 // 16 : (j0 + width) // 16]),
-                    w_sb[:, j0 : j0 + width],
-                    MULT,
+        def gather(picked, u, j0, width):
+            nc.vector.tensor_tensor(
+                picked[:, u % PACK, j0 : j0 + width],
+                planes[u][:].indirect(offsets[:, j0 // LIST_ROWS : (j0 + width) // LIST_ROWS]),
+                w_sb[:, j0 : j0 + width],
+                MULT,
+            )
+
+        def pack(picked, a, j0, width, copy, codes_slot=None):
+            rounded = keep.tile([P, PACK * width], BF16, name="xg", tag="xg%d_%d" % (a, j0), align_bytes=64)
+            copy(woven(rounded[:]), by_rows(picked[:, :, j0 : j0 + width]))
+            quantise(xq[a], "xq%d_%d" % (a, j0), rounded[:], j0, width, codes_slot)
+
+        def first_tier(part, codes_slot=None):
+            j0, width = c_parts[part]
+            rounded = keep.tile([P, PACK * width], BF16, name="cb%d" % part, align_bytes=64)
+            nc.scalar.copy(woven(rounded[:]), by_rows(c_sb[part][:]))
+            quantise(cq, "cq%d" % part, rounded[:], j0, width, codes_slot)
+
+        def values_of(j):
+            codes, scales = cq[j]
+            values = psum.tile([P, PACK, BLOCK], F32, name="values", tag="bank%d" % VALUE_BANKS[j // BLOCK % 2])
+            for t in range(PACK):
+                nc.tensor.matmul_mx(
+                    out=values[:, t, :],
+                    lhsT=eye_codes[:, t * P : (t + 1) * P].bitcast(FP8X4),
+                    lhsT_scale=eye_scales[:, t * P : (t + 1) * P],
+                    rhs=codes.bitcast(FP8X4),
+                    rhs_scale=scales,
+                    start=True,
+                    stop=True,
                 )
-            part = min(width, HALF)
-            for s0 in range(0, width, part):
-                rounded = keep.tile([P, PACK * part], BF16, name="xg", tag="xg%d_%d" % (a, j0 + s0), align_bytes=64)
-                nc.scalar.copy(woven(rounded[:]), by_rows(picked[:, :, s0 : s0 + part]))
-                codes, scales = quantised("xq%d_%d" % (a, j0 + s0), rounded[:], part)
-                for s in range(0, part, BANK_COLS):
-                    xq[(a, j0 + s0 + s)] = (codes[:, s : s + BANK_COLS], scales[:, s : s + BANK_COLS])
+            return values
 
-        def tiers(k, parts, slot, codes_slot):
-            rows = c_sb[k][:]
-            rounded = keep.tile([P, PACK * CHUNK], BF16, name="cb%d" % k, align_bytes=64)
-            nc.scalar.copy(woven(rounded[:]), by_rows(rows))
-            codes, scales = quantised("cq%d" % k, rounded[:], CHUNK, codes_slot)
-            left = keep.tile([P, PACK * CHUNK], BF16, name="left%d" % k, tag=slot, align_bytes=64)
-            for s in range(0, CHUNK, BANK_COLS):
-                cq[k * CHUNK + s] = (codes[:, s : s + BANK_COLS], scales[:, s : s + BANK_COLS])
-                back = back_psum.tile([P, PACK, BANK_COLS], F32, name="back")
-                for t in range(PACK):
-                    nc.tensor.matmul_mx(
-                        out=back[:, t, :],
-                        lhsT=eye_codes[:, t * P : (t + 1) * P].bitcast(FP8X4),
-                        lhsT_scale=eye_scales[:, t * P : (t + 1) * P],
-                        rhs=codes[:, s : s + BANK_COLS].bitcast(FP8X4),
-                        rhs_scale=scales[:, s : s + BANK_COLS],
-                        start=True,
-                        stop=True,
-                    )
+        def leftover_on_vector(part, s0):
+            left = keep.tile([P, PACK * CHUNK], BF16, name="left%d_%d" % (part, s0), align_bytes=64)
+            for s in range(0, CHUNK, BLOCK):
                 nc.vector.tensor_tensor(
-                    woven(left[:, PACK * s : PACK * (s + BANK_COLS)]),
-                    by_rows(rows[:, :, s : s + BANK_COLS]),
-                    by_rows(back[:]),
+                    woven(left[:, PACK * s : PACK * (s + BLOCK)]),
+                    by_rows(c_sb[part][:, :, s0 + s : s0 + s + BLOCK]),
+                    by_rows(values_of(c_parts[part][0] + s0 + s)[:]),
                     SUB,
                 )
-            width = CHUNK // parts
-            for s0 in range(0, CHUNK, width):
-                codes, scales = quantised("cr%d_%d" % (k, s0), left[:, PACK * s0 : PACK * (s0 + width)], width)
-                for s in range(0, width, BANK_COLS):
-                    cr[k * CHUNK + s0 + s] = (codes[:, s : s + BANK_COLS], scales[:, s : s + BANK_COLS])
+            return left
+
+        def leftover_on_tensor(part):
+            left = keep.tile([P, PACK * CHUNK], BF16, name="left%d" % part, align_bytes=64)
+            turned_back = psum.tile([P, 2, 2, BLOCK], F32, name="turned_back", tag="bank%d" % TURN_BACK_BANK)
+            for b in range(CHUNK // BLOCK):
+                s = b * BLOCK
+                negated = stage.tile([P, PACK, BLOCK], F32, name="negated")
+                nc.scalar.activation(negated[:], values_of(c_parts[part][0] + s)[:], COPY, scale=-1.0)
+                turned = psum.tile([P, PACK, P], F32, name="turned", tag="bank%d" % TURN_BANKS[b])
+                for term, (source, col) in enumerate(((c_sb[part][:], s), (negated[:], 0))):
+                    for t in range(PACK):
+                        nc.tensor.matmul(
+                            turned[:, t, :],
+                            source[:, t, col : col + BLOCK],
+                            square[:],
+                            start=(term == 0 and t == 0),
+                            stop=(term == 1 and t == PACK - 1),
+                            is_transpose=True,
+                        )
+                pairs = stage.tile([P, PACK * P], BF16, name="pairs")
+                nc.scalar.copy(
+                    pairs[:].rearrange("j (u p e) -> j u p e", u=2, e=2),
+                    turned[:].rearrange("j (u e) p -> j u p e", u=2),
+                )
+                for u in range(2):
+                    nc.tensor.transpose(turned_back[:, b, u, :], pairs[:].bitcast(F32)[:, u * P : (u + 1) * P], square[:])
+            nc.scalar.copy(
+                left[:].bitcast(F32).rearrange("p (b j u) -> p b j u", b=2, u=2),
+                turned_back[:].rearrange("p b u j -> p b j u"),
+            )
+            return left
+
+        def second_tier(j0, left, width, codes_slot=None):
+            for s in range(0, CHUNK, width):
+                quantise(cr, "cr%d" % (j0 + s), left[:, PACK * s : PACK * (s + width)], j0 + s, width, codes_slot)
 
         y_codes = keep.tile([P, J], U32, name="y_codes", align_bytes=64)
         y_scales = keep.tile([P, J], U8, name="y_scales", align_bytes=64)
         y_rows = out_0.rearrange("(p t) j -> p t j", t=PACK)
         words_out = out_1[0].rearrange("p j i -> p (j i)").bitcast(I32)
 
-        def project(j0, width, order, drain):
+        def project(j0, order, drains):
+            width = BLOCK * len(drains)
             y_sb = keep.tile([P, PACK, width], F32, name="y%d" % j0)
             rounded = keep.tile([P, PACK * width], BF16, name="yb%d" % j0, align_bytes=64)
-            for s in range(0, width, BANK_COLS):
-                acc = y_psum.tile([P, PACK, BANK_COLS], F32, name="acc")
+            for b, drain in enumerate(drains):
+                s = b * BLOCK
                 j = j0 + s
-                operands = (cq[j], cr[j], xq[(0, j)], xq[(1, j)])
-                for step in order:
-                    codes, scales = operands[step]
+                acc = psum.tile([P, PACK, BLOCK], F32, name="acc", tag="bank%d" % Y_BANKS[j // BLOCK])
+                moving = (cq[j], cr[j], xq[0][j], xq[1][j])
+                for term in order:
+                    codes, scales = moving[term]
                     for t in range(PACK):
                         cols = slice(t * P, (t + 1) * P)
-                        if step < 2:
-                            lhs = wx_dealt[:, 2 * t * P : 2 * (t + 1) * P].bitcast(FP4X4)
-                            lhs_scale = scales_dealt[:, cols]
+                        if term < 2:
+                            weights = wx_dealt[:, 2 * t * P : 2 * (t + 1) * P].bitcast(FP4X4)
+                            weight_scales = scales_dealt[:, cols]
                         else:
-                            lhs = wt_dealt[:, step - 2, cols].bitcast(FP8X4)
-                            lhs_scale = scales_dealt[4 * (step - 1) : P, cols]
+                            weights = wt_dealt[:, term - 2, cols].bitcast(FP8X4)
+                            weight_scales = scales_dealt[4 * (term - 1) : P, cols]
                         nc.tensor.matmul_mx(
                             out=acc[:, t, :],
-                            lhsT=lhs,
-                            lhsT_scale=lhs_scale,
+                            lhsT=weights,
+                            lhsT_scale=weight_scales,
                             rhs=codes.bitcast(FP8X4),
                             rhs_scale=scales,
-                            start=(step == order[0] and t == 0),
-                            stop=(step == order[3] and t == PACK - 1),
+                            start=(term == order[0] and t == 0),
+                            stop=(term == order[-1] and t == PACK - 1),
                         )
-                nc.scalar.copy(woven(rounded[:, PACK * s : PACK * (s + BANK_COLS)]), by_rows(acc[:]))
-                drain(y_sb[:, :, s : s + BANK_COLS], acc[:])
+                nc.scalar.copy(
+                    rounded[:, PACK * s : PACK * (s + BLOCK)].rearrange("p (j t) -> p j t", t=PACK),
+                    acc[:].rearrange("p t j -> p j t"),
+                )
+                drain(y_sb[:, :, s : s + BLOCK], acc[:])
             cols = slice(j0, j0 + width)
             nc.vector.quantize_mx(out=y_codes[:, cols].bitcast(FP8X4), scales=y_scales[:, cols], in_=rounded[:])
             nc.sync.dma_start(y_rows[:, :, cols], y_sb[:])
             nc.sync.dma_start(words_out[:, cols], y_codes[:, cols].bitcast(I32))
 
-        pick(0, 0, J, "wide")
-        tiers(0, 1, "plane1", None)
-        tiers(1, 1, "plane3", None)
-        pick(1, 0, CHUNK, "even")
-        pick(1, CHUNK, CHUNK, "odd")
-        project(0, CHUNK, (0, 1, 2, 3), nc.scalar.copy)
-        project(CHUNK, CHUNK, (0, 1, 2, 3), nc.scalar.copy)
-        pick(1, 512, CHUNK, "even")
-        pick(1, 768, CHUNK, "odd")
-        tiers(2, 1, "left2", "xg1_0")
-        tiers(3, 2, "left3", "xg1_256")
-        project(512, 256, (2, 3, 0, 1), nc.scalar.copy)
-        project(768, 128, (2, 3, 0, 1), nc.vector.tensor_copy)
-        project(896, 128, (2, 3, 0, 1), nc.vector.tensor_copy)
+        on_scalar, on_vector = nc.scalar.copy, nc.vector.tensor_copy
+
+        first_tier(0)
+        second_tier(0, leftover_on_tensor(0), CHUNK, "plane3")
+        first_tier(1, "plane2")
+        second_tier(CHUNK, leftover_on_tensor(1), CHUNK, "plane6")
+
+        first = gathered.tile([P, PACK, J], F32, name="first")
+        for u in range(PACK):
+            gather(first, u, 0, J)
+        pack(first, 0, 0, HALF, on_scalar, "plane5")
+
+        second = gathered.tile([P, PACK, J], F32, name="second")
+        for u in range(PACK, 2 * PACK - 1):
+            gather(second, u, 0, J)
+        for j0 in range(0, J, CHUNK):
+            gather(second, 2 * PACK - 1, j0, CHUNK)
+        pack(second, 1, 0, CHUNK, on_scalar)
+        pack(first, 0, HALF, HALF, on_scalar, "xg1_0")
+        pack(second, 1, CHUNK, CHUNK, on_scalar)
+        first_tier(2, "plane7")
+
+        project(0, PICKS_LAST, (on_scalar, on_scalar))
+        pack(second, 1, 2 * CHUNK, CHUNK, on_vector)
+        second_tier(2 * CHUNK, leftover_on_vector(2, 0), CHUNK)
+        project(CHUNK, PICKS_LAST, (on_scalar, on_scalar))
+        pack(second, 1, 3 * CHUNK, CHUNK, on_vector)
+        second_tier(3 * CHUNK, leftover_on_vector(2, CHUNK), BLOCK)
+        project(2 * CHUNK, TIERS_LAST, (on_scalar, on_scalar))
+        project(3 * CHUNK, TIERS_LAST, (on_vector,))
+        project(3 * CHUNK + BLOCK, TIERS_LAST, (on_scalar,))
+
         for q in range(4):
             queue = nc.scalar if q % 2 else nc.sync
             queue.dma_start(

@@ -1,7 +1,7 @@
+import math
 from contextlib import ExitStack
 
 import concourse.mybir as mybir
-from concourse.masks import make_identity
 
 K, L, N, T, J = 1024, 512, 512, 2048, 1024
 FLOPS = 2 * N * J * (K + 3 * L)
@@ -15,7 +15,9 @@ U8 = mybir.dt.uint8
 FP8X4 = mybir.dt.float8_e4m3fn_x4
 FP4X4 = mybir.dt.float4_e2m1fn_x4
 MULT = mybir.AluOpType.mult
+ADD = mybir.AluOpType.add
 SUB = mybir.AluOpType.subtract
+EQUAL = mybir.AluOpType.is_equal
 COPY = mybir.ActivationFunctionType.Copy
 
 P = 128
@@ -30,9 +32,6 @@ VALUE_BANKS = (4, 5)
 TURN_BANKS = (6, 7)
 TURN_BACK_BANK = 3
 Y_BANKS = (0, 1, 2, 3, 6, 7, 0, 1)
-
-PICKS_LAST = (0, 1, 2, 3)
-TIERS_LAST = (2, 3, 0, 1)
 
 
 def woven(ap):
@@ -53,9 +52,24 @@ def tile_list_noneP_kernel(
         psum = ctx.enter_context(tc.psum_pool(name="psum", bufs=1))
         stage = ctx.enter_context(tc.tile_pool(name="stage", bufs=2))
 
+        shared = ctx.enter_context(tc.tile_pool(name="shared", bufs=1))
+        starts = {}
+
+        def host(name, shape, before=0, spare=0):
+            starts[name] = starts.get("end", 0) + before
+            starts["end"] = starts[name] + 4 * math.prod(shape[1:]) + spare
+            return shared.tile(shape, F32, name=name, offset=starts[name], align_bytes=64)
+
+        def guest(name, shape, dtype, slot):
+            if slot is None:
+                return keep.tile(shape, dtype, name=name, align_bytes=64)
+            return shared.tile(shape, dtype, name=name, offset=starts[slot[0]] + slot[1], align_bytes=64)
+
         offsets = keep.tile([P, J // LIST_ROWS], U16, name="offsets")
         nc.sync.dma_start(offsets[:], offs)
 
+        c_first = host("c0", [P, PACK, CHUNK])
+        nc.sync.dma_start(c_first[:], c.rearrange("(p t) j -> p t j", t=PACK)[:, :, :CHUNK])
         wx_raw = keep.tile([P, 2 * N], U8, name="wx_raw", align_bytes=64)
         nc.sync.dma_start(wx_raw[:].bitcast(I32), wx_words[0].bitcast(I32))
         wt_raw = keep.tile([P, 2, N], I32, name="wt_raw", align_bytes=64)
@@ -65,9 +79,18 @@ def tile_list_noneP_kernel(
         nc.vector.memset(scales_raw[:].bitcast(I32), 0)
 
         square = keep.tile([P, P], F32, name="square")
-        make_identity(nc, square[:])
+        ones = keep.tile([P, P], F32, name="ones")
+        nc.vector.memset(ones[:], 1.0)
+        column = keep.tile([P, P], F32, name="column", align_bytes=64)
+        nc.vector.tensor_tensor_scan(column[:], ones[:], ones[:], -1.0, MULT, ADD)
+        in_group = keep.tile([P, 32], F32, name="in_group", align_bytes=64)
+        nc.vector.transpose(in_group[:], column[:, :32])
+        group_start = keep.tile([P, 1], F32, name="group_start")
+        for q in range(4):
+            nc.vector.memset(group_start[32 * q : 32 * (q + 1), :], 32.0 * q)
+        nc.vector.tensor_scalar(square[:], column[:], group_start[:], in_group[:, 0:1], SUB, EQUAL)
         eye = keep.tile([P, PACK * P * PACK], BF16, name="eye", align_bytes=64)
-        nc.vector.memset(eye[:], 0.0)
+        nc.vector.memset(eye[:].bitcast(I32), 0)
         for t in range(PACK):
             nc.vector.tensor_copy(eye[:, PACK * P * t + t : PACK * P * (t + 1) : PACK], square[:])
 
@@ -80,9 +103,9 @@ def tile_list_noneP_kernel(
             )
 
         w_sb = keep.tile([P, J], F32, name="w_sb")
-        planes = [keep.tile([P, T], F32, name="plane%d" % u, align_bytes=64) for u in range(2 * PACK)]
-        c_parts = ((0, CHUNK), (CHUNK, CHUNK), (HALF, HALF))
-        c_sb = [keep.tile([P, PACK, width], F32, name="c%d" % j0) for j0, width in c_parts]
+        planes = [host("plane%d" % u, [P, T]) for u in range(2 * PACK)]
+        c_parts = tuple((j0, CHUNK) for j0 in range(0, J, CHUNK))
+        c_sb = [c_first] + [host("c%d" % j0, [P, PACK, width], 4096, 4096) for j0, width in c_parts[1:]]
         x_rows = xT.rearrange("(a p t) s -> a t p s", a=2, t=PACK)
         c_rows = c.rearrange("(p t) j -> p t j", t=PACK)
 
@@ -93,17 +116,23 @@ def tile_list_noneP_kernel(
             j0, width = c_parts[part]
             nc.sync.dma_start(c_sb[part][:], c_rows[:, :, j0 : j0 + width])
 
-        nc.sync.dma_start(w_sb[:], wgt)
+        nc.sync.dma_start(w_sb[:, :HALF], wgt[:, :HALF])
         load_plane(0)
-        load_c(0)
+        nc.sync.dma_start(w_sb[:, HALF:], wgt[:, HALF:])
         load_plane(1)
         load_c(1)
-        for q in range(4):
-            load_scales(q)
-            load_plane(2 + q)
+        load_scales(0)
+        load_plane(2)
+        load_scales(1)
+        load_plane(3)
         load_c(2)
+        load_scales(2)
+        load_plane(4)
+        load_scales(3)
+        load_plane(5)
         load_plane(6)
         load_plane(7)
+        load_c(3)
 
         wx_dealt = keep.tile([P, 2 * N], U8, name="wx_dealt", align_bytes=64)
         nc.vector.tensor_copy(
@@ -129,30 +158,41 @@ def tile_list_noneP_kernel(
         cr = {}
 
         def quantise(into, name, src, j0, width, slot=None):
-            codes = keep.tile([P, width], U32, name=name + "_codes", tag=slot or name, align_bytes=64)
+            codes = guest(name + "_codes", [P, width], U32, slot)
             scales = keep.tile([P, width], U8, name=name + "_scales", align_bytes=64)
             nc.vector.quantize_mx(out=codes[:].bitcast(FP8X4), scales=scales[:], in_=src)
             for s in range(0, width, BLOCK):
                 into[j0 + s] = (codes[:, s : s + BLOCK], scales[:, s : s + BLOCK])
 
-        def gather(picked, u, j0, width):
+        def gather(picked, u, j0, width, base=0):
             nc.vector.tensor_tensor(
-                picked[:, u % PACK, j0 : j0 + width],
+                picked[:, u % PACK, j0 - base : j0 - base + width],
                 planes[u][:].indirect(offsets[:, j0 // LIST_ROWS : (j0 + width) // LIST_ROWS]),
                 w_sb[:, j0 : j0 + width],
                 MULT,
             )
 
-        def pack(picked, a, j0, width, copy, codes_slot=None):
-            rounded = keep.tile([P, PACK * width], BF16, name="xg", tag="xg%d_%d" % (a, j0), align_bytes=64)
-            copy(woven(rounded[:]), by_rows(picked[:, :, j0 : j0 + width]))
+        xg = {}
+        cb = {}
+
+        def weave_x(picked, a, j0, width, copy, base=0, into=None):
+            if into is None:
+                into = keep.tile([P, PACK * width], BF16, name="xg", tag="xg%d_%d" % (a, j0), align_bytes=64)
+            rounded = into
+            copy(woven(rounded[:]), by_rows(picked[:, :, j0 - base : j0 - base + width]))
+            xg[a, j0] = (rounded, width)
+
+        def quantise_x(a, j0, codes_slot=None):
+            rounded, width = xg[a, j0]
             quantise(xq[a], "xq%d_%d" % (a, j0), rounded[:], j0, width, codes_slot)
 
-        def first_tier(part, codes_slot=None):
-            j0, width = c_parts[part]
-            rounded = keep.tile([P, PACK * width], BF16, name="cb%d" % part, align_bytes=64)
+        def weave_c(part, slot=None):
+            rounded = guest("cb%d" % part, [P, PACK * CHUNK], BF16, slot)
             nc.scalar.copy(woven(rounded[:]), by_rows(c_sb[part][:]))
-            quantise(cq, "cq%d" % part, rounded[:], j0, width, codes_slot)
+            cb[part] = rounded
+
+        def first_tier(part, codes_slot=None):
+            quantise(cq, "cq%d" % part, cb[part][:], part * CHUNK, CHUNK, codes_slot)
 
         def values_of(j):
             codes, scales = cq[j]
@@ -180,8 +220,8 @@ def tile_list_noneP_kernel(
                 )
             return left
 
-        def leftover_on_tensor(part):
-            left = keep.tile([P, PACK * CHUNK], BF16, name="left%d" % part, align_bytes=64)
+        def leftover_on_tensor(part, slot=None):
+            left = guest("left%d" % part, [P, PACK * CHUNK], BF16, slot)
             turned_back = psum.tile([P, 2, 2, BLOCK], F32, name="turned_back", tag="bank%d" % TURN_BACK_BANK)
             for b in range(CHUNK // BLOCK):
                 s = b * BLOCK
@@ -220,75 +260,162 @@ def tile_list_noneP_kernel(
         y_rows = out_0.rearrange("(p t) j -> p t j", t=PACK)
         words_out = out_1[0].rearrange("p j i -> p (j i)").bitcast(I32)
 
-        def project(j0, order, drains):
-            width = BLOCK * len(drains)
-            y_sb = keep.tile([P, PACK, width], F32, name="y%d" % j0)
-            rounded = keep.tile([P, PACK * width], BF16, name="yb%d" % j0, align_bytes=64)
-            for b, drain in enumerate(drains):
-                s = b * BLOCK
-                j = j0 + s
-                acc = psum.tile([P, PACK, BLOCK], F32, name="acc", tag="bank%d" % Y_BANKS[j // BLOCK])
-                moving = (cq[j], cr[j], xq[0][j], xq[1][j])
-                for term in order:
-                    codes, scales = moving[term]
-                    for t in range(PACK):
-                        cols = slice(t * P, (t + 1) * P)
-                        if term < 2:
-                            weights = wx_dealt[:, 2 * t * P : 2 * (t + 1) * P].bitcast(FP4X4)
-                            weight_scales = scales_dealt[:, cols]
-                        else:
-                            weights = wt_dealt[:, term - 2, cols].bitcast(FP8X4)
-                            weight_scales = scales_dealt[4 * (term - 1) : P, cols]
-                        nc.tensor.matmul_mx(
-                            out=acc[:, t, :],
-                            lhsT=weights,
-                            lhsT_scale=weight_scales,
-                            rhs=codes.bitcast(FP8X4),
-                            rhs_scale=scales,
-                            start=(term == order[0] and t == 0),
-                            stop=(term == order[-1] and t == PACK - 1),
-                        )
-                nc.scalar.copy(
-                    rounded[:, PACK * s : PACK * (s + BLOCK)].rearrange("p (j t) -> p j t", t=PACK),
-                    acc[:].rearrange("p t j -> p j t"),
-                )
-                drain(y_sb[:, :, s : s + BLOCK], acc[:])
-            cols = slice(j0, j0 + width)
+        sums = {}
+        done = {}
+
+        def add_terms(b, terms):
+            j = b * BLOCK
+            if b not in sums:
+                sums[b] = psum.tile([P, PACK, BLOCK], F32, name="acc", tag="bank%d" % Y_BANKS[b])
+                done[b] = []
+            for term in terms:
+                done[b].append(term)
+                codes, scales = (cq, cr, xq[0], xq[1])[term][j]
+                for t in range(PACK):
+                    cols = slice(t * P, (t + 1) * P)
+                    if term < 2:
+                        weights = wx_dealt[:, 2 * t * P : 2 * (t + 1) * P].bitcast(FP4X4)
+                        weight_scales = scales_dealt[:, cols]
+                    else:
+                        weights = wt_dealt[:, term - 2, cols].bitcast(FP8X4)
+                        weight_scales = scales_dealt[4 * (term - 1) : P, cols]
+                    nc.tensor.matmul_mx(
+                        out=sums[b][:, t, :],
+                        lhsT=weights,
+                        lhsT_scale=weight_scales,
+                        rhs=codes.bitcast(FP8X4),
+                        rhs_scale=scales,
+                        start=(term == 0 and t == 0),
+                        stop=(len(done[b]) == 4 and t == PACK - 1),
+                    )
+
+        y_rounded = {}
+
+        y_float = {}
+
+        def open_y(b0, blocks):
+            y_float[b0] = keep.tile([P, PACK, BLOCK * blocks], F32, name="y%d" % b0)
+            y_rounded[b0] = (keep.tile([P, PACK * BLOCK * blocks], BF16, name="yb%d" % b0, align_bytes=64), BLOCK * blocks)
+
+        def copy_y(b0, b, copy):
+            s = (b - b0) * BLOCK
+            copy(y_float[b0][:, :, s : s + BLOCK], sums[b][:])
+
+        def round_y(b0, b):
+            s = (b - b0) * BLOCK
+            nc.scalar.copy(
+                y_rounded[b0][0][:, PACK * s : PACK * (s + BLOCK)].rearrange("p (j t) -> p j t", t=PACK),
+                sums[b][:].rearrange("p t j -> p j t"),
+            )
+
+        def round_copied_y(b0, b, blocks=1):
+            s = (b - b0) * BLOCK
+            width = BLOCK * blocks
+            nc.vector.tensor_copy(
+                woven(y_rounded[b0][0][:, PACK * s : PACK * (s + width)]), by_rows(y_float[b0][:, :, s : s + width])
+            )
+
+        def store_y(b0):
+            width = y_rounded[b0][1]
+            nc.sync.dma_start(y_rows[:, :, b0 * BLOCK : b0 * BLOCK + width], y_float[b0][:])
+
+        def drain(b0, blocks):
+            open_y(b0, blocks)
+            for b in range(b0, b0 + blocks):
+                round_y(b0, b)
+                copy_y(b0, b, nc.scalar.copy)
+            store_y(b0)
+
+        def quantise_y(b0):
+            rounded, width = y_rounded[b0]
+            cols = slice(b0 * BLOCK, b0 * BLOCK + width)
             nc.vector.quantize_mx(out=y_codes[:, cols].bitcast(FP8X4), scales=y_scales[:, cols], in_=rounded[:])
-            nc.sync.dma_start(y_rows[:, :, cols], y_sb[:])
             nc.sync.dma_start(words_out[:, cols], y_codes[:, cols].bitcast(I32))
 
         on_scalar, on_vector = nc.scalar.copy, nc.vector.tensor_copy
 
-        first_tier(0)
-        second_tier(0, leftover_on_tensor(0), CHUNK, "plane3")
-        first_tier(1, "plane2")
-        second_tier(CHUNK, leftover_on_tensor(1), CHUNK, "plane6")
-
+        EARLY = 3 * BLOCK
+        LATE = 5 * BLOCK
         first = gathered.tile([P, PACK, J], F32, name="first")
-        for u in range(PACK):
+        early = host("early", [P, PACK, EARLY])
+        middle = gathered.tile([P, PACK * CHUNK], F32, name="middle", align_bytes=64)
+        late = gathered.tile([P, PACK * (J - LATE)], F32, name="late", align_bytes=64)
+        middle_rows = middle[:].rearrange("p (t j) -> p t j", t=PACK)
+        late_rows = late[:].rearrange("p (t j) -> p t j", t=PACK)
+        gather(first, 0, 0, HALF)
+        gather(first, 0, HALF, HALF)
+        for u in range(1, PACK):
             gather(first, u, 0, J)
-        pack(first, 0, 0, HALF, on_scalar, "plane5")
-
-        second = gathered.tile([P, PACK, J], F32, name="second")
-        for u in range(PACK, 2 * PACK - 1):
-            gather(second, u, 0, J)
-        for j0 in range(0, J, CHUNK):
-            gather(second, 2 * PACK - 1, j0, CHUNK)
-        pack(second, 1, 0, CHUNK, on_scalar)
-        pack(first, 0, HALF, HALF, on_scalar, "xg1_0")
-        pack(second, 1, CHUNK, CHUNK, on_scalar)
-        first_tier(2, "plane7")
-
-        project(0, PICKS_LAST, (on_scalar, on_scalar))
-        pack(second, 1, 2 * CHUNK, CHUNK, on_vector)
-        second_tier(2 * CHUNK, leftover_on_vector(2, 0), CHUNK)
-        project(CHUNK, PICKS_LAST, (on_scalar, on_scalar))
-        pack(second, 1, 3 * CHUNK, CHUNK, on_vector)
-        second_tier(3 * CHUNK, leftover_on_vector(2, CHUNK), BLOCK)
-        project(2 * CHUNK, TIERS_LAST, (on_scalar, on_scalar))
-        project(3 * CHUNK, TIERS_LAST, (on_vector,))
-        project(3 * CHUNK + BLOCK, TIERS_LAST, (on_scalar,))
+        for u in (4, 5):
+            gather(early, u, 0, EARLY)
+            gather(middle_rows, u, EARLY, CHUNK, EARLY)
+            gather(late_rows, u, LATE, J - LATE, LATE)
+        gather(early, 6, 0, EARLY)
+        weave_c(0)
+        first_tier(0)
+        left0 = leftover_on_tensor(0)
+        weave_c(1)
+        first_tier(1)
+        second_tier(0, left0, CHUNK, ("c256", 0))
+        left1 = leftover_on_tensor(1, ("c512", 64))
+        weave_c(2)
+        first_tier(2)
+        second_tier(CHUNK, left1, CHUNK, ("plane4", 2048))
+        weave_x(first, 0, 0, HALF, on_scalar, 0, guest("xg_a", [P, PACK * HALF], BF16, ("c512", 2112)))
+        quantise_x(0, 0, ("plane4", 0))
+        left2 = leftover_on_tensor(2)
+        xg_b = guest("xg_b", [P, PACK * HALF], BF16, ("c512", 64 - 4096))
+        for s in (0, CHUNK):
+            nc.scalar.copy(woven(xg_b[:, PACK * s : PACK * (s + CHUNK)]), by_rows(first[:, :, HALF + s : HALF + s + CHUNK]))
+        xg[0, HALF] = (xg_b, HALF)
+        for b in range(4):
+            add_terms(b, (0, 1, 2))
+        gather(early, 7, 0, BLOCK)
+        gather(early, 7, BLOCK, CHUNK)
+        weave_x(early, 1, 0, BLOCK, on_scalar, 0, middle[:, 2 * CHUNK : 3 * CHUNK].bitcast(BF16))
+        weave_x(early, 1, BLOCK, CHUNK, on_scalar, 0, late[:, 4 * CHUNK : 6 * CHUNK].bitcast(BF16))
+        quantise_x(1, 0)
+        add_terms(0, (3,))
+        gather(middle_rows, 6, EARLY, CHUNK, EARLY)
+        gather(middle_rows, 7, EARLY, CHUNK, EARLY)
+        quantise_x(1, BLOCK)
+        add_terms(1, (3,))
+        add_terms(2, (3,))
+        weave_c(3)
+        drain(0, 2)
+        weave_x(middle_rows, 1, EARLY, CHUNK, on_vector, EARLY)
+        quantise_x(0, HALF, ("early", 0))
+        quantise_x(1, EARLY)
+        second_tier(2 * CHUNK, left2, CHUNK, ("early", 2048))
+        add_terms(3, (3,))
+        add_terms(4, (0, 2, 1, 3))
+        drain(2, 2)
+        gather(late_rows, 6, LATE, J - LATE, LATE)
+        gather(late_rows, 7, LATE, CHUNK, LATE)
+        first_tier(3)
+        weave_x(late_rows, 1, LATE, CHUNK, on_vector, LATE)
+        gather(late_rows, 7, 7 * BLOCK, BLOCK, LATE)
+        quantise_x(1, LATE)
+        add_terms(5, (0, 2, 1, 3))
+        drain(4, 2)
+        weave_x(late_rows, 1, 7 * BLOCK, BLOCK, on_vector, LATE)
+        second_tier(3 * CHUNK, leftover_on_vector(3, 0), BLOCK)
+        quantise_x(1, 7 * BLOCK)
+        add_terms(6, (0, 2, 3, 1))
+        add_terms(7, (0, 2, 3, 1))
+        quantise_y(0)
+        quantise_y(2)
+        quantise_y(4)
+        open_y(6, 1)
+        open_y(7, 1)
+        round_y(6, 6)
+        copy_y(6, 6, on_vector)
+        store_y(6)
+        copy_y(7, 7, on_scalar)
+        store_y(7)
+        round_y(7, 7)
+        quantise_y(6)
+        quantise_y(7)
 
         for q in range(4):
             queue = nc.scalar if q % 2 else nc.sync

@@ -68,6 +68,10 @@ def tile_list_noneP_kernel(
         offsets = keep.tile([P, J // LIST_ROWS], U16, name="offsets")
         nc.sync.dma_start(offsets[:], offs)
 
+        w_rows = keep.tile([P, P], F32, name="w_rows")
+        nc.sync.dma_start(
+            w_rows[:], wgt.rearrange("(g r) j -> g (r j)", r=LIST_ROWS)[:, : 2 * J].rearrange("g (q c) -> g q c", c=P)
+        )
         c_first = host("c0", [P, PACK, CHUNK])
         nc.sync.dma_start(c_first[:], c.rearrange("(p t) j -> p t j", t=PACK)[:, :, :CHUNK])
         wx_raw = keep.tile([P, 2 * N], U8, name="wx_raw", align_bytes=64)
@@ -116,23 +120,32 @@ def tile_list_noneP_kernel(
             j0, width = c_parts[part]
             nc.sync.dma_start(c_sb[part][:], c_rows[:, :, j0 : j0 + width])
 
-        nc.sync.dma_start(w_sb[:, :HALF], wgt[:, :HALF])
         load_plane(0)
-        nc.sync.dma_start(w_sb[:, HALF:], wgt[:, HALF:])
         load_plane(1)
         load_c(1)
         load_scales(0)
         load_plane(2)
         load_scales(1)
         load_plane(3)
-        load_c(2)
         load_scales(2)
-        load_plane(4)
+        load_c(2)
         load_scales(3)
-        load_plane(5)
-        load_plane(6)
-        load_plane(7)
+        for u in range(4, 8):
+            load_plane(u)
         load_c(3)
+
+        w_turned = psum.tile([P, P], F32, name="w_turned", tag="bank2")
+        nc.tensor.transpose(w_turned[:], w_rows[:], square[:])
+        w_wide = keep.tile([P, J], F32, name="w_wide")
+        nc.scalar.copy(
+            w_wide[:].rearrange("c (b g i) -> c b g i", g=8, i=LIST_ROWS),
+            w_turned[:].rearrange("c (g q) -> c q g", q=LIST_ROWS)[:, :8, :].unsqueeze(3).to_broadcast([P, 8, 8, LIST_ROWS]),
+        )
+        for h in range(2):
+            w_back = psum.tile([P, HALF], F32, name="w_back", tag="bank%d" % h)
+            for s in range(0, HALF, P):
+                nc.tensor.transpose(w_back[:, s : s + P], w_wide[:, h * HALF + s : h * HALF + s + P], square[:])
+            nc.scalar.copy(w_sb[:, h * HALF : (h + 1) * HALF], w_back[:])
 
         wx_dealt = keep.tile([P, 2 * N], U8, name="wx_dealt", align_bytes=64)
         nc.vector.tensor_copy(
@@ -322,14 +335,27 @@ def tile_list_noneP_kernel(
         def drain(b0, blocks):
             open_y(b0, blocks)
             for b in range(b0, b0 + blocks):
-                round_y(b0, b)
                 copy_y(b0, b, nc.scalar.copy)
             store_y(b0)
+            for b in range(b0, b0 + blocks):
+                round_y(b0, b)
 
         def quantise_y(b0):
             rounded, width = y_rounded[b0]
             cols = slice(b0 * BLOCK, b0 * BLOCK + width)
             nc.vector.quantize_mx(out=y_codes[:, cols].bitcast(FP8X4), scales=y_scales[:, cols], in_=rounded[:])
+
+        def quantise_part(b0, b, blocks):
+            s = PACK * (b - b0) * BLOCK
+            cols = slice(b * BLOCK, (b + blocks) * BLOCK)
+            nc.vector.quantize_mx(
+                out=y_codes[:, cols].bitcast(FP8X4),
+                scales=y_scales[:, cols],
+                in_=y_rounded[b0][0][:, s : s + PACK * blocks * BLOCK],
+            )
+
+        def store_words(b0, blocks):
+            cols = slice(b0 * BLOCK, (b0 + blocks) * BLOCK)
             nc.sync.dma_start(words_out[:, cols], y_codes[:, cols].bitcast(I32))
 
         on_scalar, on_vector = nc.scalar.copy, nc.vector.tensor_copy
@@ -342,9 +368,7 @@ def tile_list_noneP_kernel(
         late = gathered.tile([P, PACK * (J - LATE)], F32, name="late", align_bytes=64)
         middle_rows = middle[:].rearrange("p (t j) -> p t j", t=PACK)
         late_rows = late[:].rearrange("p (t j) -> p t j", t=PACK)
-        gather(first, 0, 0, HALF)
-        gather(first, 0, HALF, HALF)
-        for u in range(1, PACK):
+        for u in range(PACK):
             gather(first, u, 0, J)
         for u in (4, 5):
             gather(early, u, 0, EARLY)
@@ -382,40 +406,51 @@ def tile_list_noneP_kernel(
         add_terms(1, (3,))
         add_terms(2, (3,))
         weave_c(3)
-        drain(0, 2)
-        weave_x(middle_rows, 1, EARLY, CHUNK, on_vector, EARLY)
+        weave_x(middle_rows, 1, EARLY, CHUNK, on_scalar, EARLY)
         quantise_x(0, HALF, ("early", 0))
-        quantise_x(1, EARLY)
         second_tier(2 * CHUNK, left2, CHUNK, ("early", 2048))
+        gather(late_rows, 6, LATE, J - LATE, LATE)
+        quantise_x(1, EARLY)
         add_terms(3, (3,))
         add_terms(4, (0, 2, 1, 3))
-        drain(2, 2)
-        gather(late_rows, 6, LATE, J - LATE, LATE)
-        gather(late_rows, 7, LATE, CHUNK, LATE)
         first_tier(3)
+        gather(late_rows, 7, LATE, J - LATE, LATE)
         weave_x(late_rows, 1, LATE, CHUNK, on_vector, LATE)
-        gather(late_rows, 7, 7 * BLOCK, BLOCK, LATE)
+        left3 = leftover_on_vector(3, 0)
         quantise_x(1, LATE)
         add_terms(5, (0, 2, 1, 3))
-        drain(4, 2)
         weave_x(late_rows, 1, 7 * BLOCK, BLOCK, on_vector, LATE)
-        second_tier(3 * CHUNK, leftover_on_vector(3, 0), BLOCK)
+        second_tier(3 * CHUNK, left3, CHUNK)
         quantise_x(1, 7 * BLOCK)
+        open_y(0, 2)
+        open_y(2, 3)
+        open_y(5, 1)
+        open_y(6, 2)
+        for b in range(5):
+            copy_y(0 if b < 2 else 2, b, on_scalar)
+            if b in (1, 4):
+                store_y(0 if b < 2 else 2)
+        for b in range(2, 5):
+            round_y(2, b)
         add_terms(6, (0, 2, 3, 1))
-        add_terms(7, (0, 2, 3, 1))
-        quantise_y(0)
-        quantise_y(2)
-        quantise_y(4)
-        open_y(6, 1)
-        open_y(7, 1)
-        round_y(6, 6)
-        copy_y(6, 6, on_vector)
+        add_terms(7, (0, 2, 1, 3))
+        quantise_part(2, 2, 2)
+        quantise_part(2, 4, 1)
+        store_words(2, 3)
+        copy_y(5, 5, on_scalar)
+        store_y(5)
+        copy_y(6, 6, on_scalar)
+        copy_y(6, 7, on_scalar)
         store_y(6)
-        copy_y(7, 7, on_scalar)
-        store_y(7)
-        round_y(7, 7)
-        quantise_y(6)
-        quantise_y(7)
+        round_copied_y(0, 0, 2)
+        round_copied_y(5, 5)
+        quantise_part(0, 0, 2)
+        store_words(0, 2)
+        quantise_part(5, 5, 1)
+        round_copied_y(6, 6)
+        round_y(6, 7)
+        quantise_part(6, 6, 2)
+        store_words(5, 3)
 
         for q in range(4):
             queue = nc.scalar if q % 2 else nc.sync

@@ -29,7 +29,7 @@ HALF = 512
 RUN = 4
 
 VALUE_BANKS = (4, 5)
-TURN_BANKS = (6, 7)
+TURN_BANKS = ((6, 7), (0, 1))
 TURN_BACK_BANK = 3
 Y_BANKS = (0, 1, 2, 3, 6, 7, 0, 1)
 
@@ -77,7 +77,6 @@ def tile_list_noneP_kernel(
         wx_raw = keep.tile([P, 2 * N], U8, name="wx_raw", align_bytes=64)
         nc.sync.dma_start(wx_raw[:].bitcast(I32), wx_words[0].bitcast(I32))
         wt_raw = keep.tile([P, 2, N], I32, name="wt_raw", align_bytes=64)
-        nc.sync.dma_start(wt_raw[:], wt_words.rearrange("a p n i -> p a (n i)").bitcast(I32))
 
         scales_raw = keep.tile([P, N], U8, name="scales_raw", align_bytes=64)
         nc.vector.memset(scales_raw[:].bitcast(I32), 0)
@@ -130,7 +129,9 @@ def tile_list_noneP_kernel(
         load_scales(2)
         load_c(2)
         load_scales(3)
-        for u in range(4, 8):
+        load_plane(4)
+        nc.sync.dma_start(wt_raw[:], wt_words.rearrange("a p n i -> p a (n i)").bitcast(I32))
+        for u in range(5, 8):
             load_plane(u)
         load_c(3)
 
@@ -240,7 +241,7 @@ def tile_list_noneP_kernel(
                 s = b * BLOCK
                 negated = stage.tile([P, PACK, BLOCK], F32, name="negated")
                 nc.scalar.activation(negated[:], values_of(c_parts[part][0] + s)[:], COPY, scale=-1.0)
-                turned = psum.tile([P, PACK, P], F32, name="turned", tag="bank%d" % TURN_BANKS[b])
+                turned = psum.tile([P, PACK, P], F32, name="turned", tag="bank%d" % TURN_BANKS[part % 2][b])
                 for term, (source, col) in enumerate(((c_sb[part][:], s), (negated[:], 0))):
                     for t in range(PACK):
                         nc.tensor.matmul(
@@ -377,15 +378,15 @@ def tile_list_noneP_kernel(
         gather(early, 6, 0, EARLY)
         weave_c(0)
         first_tier(0)
-        left0 = leftover_on_tensor(0)
+        left0 = leftover_on_tensor(0, ("c256", 0))
         weave_c(1)
         first_tier(1)
-        second_tier(0, left0, CHUNK, ("c256", 0))
+        second_tier(0, left0, CHUNK, ("c512", 2112))
         left1 = leftover_on_tensor(1, ("c512", 64))
         weave_c(2)
         first_tier(2)
         second_tier(CHUNK, left1, CHUNK, ("plane4", 2048))
-        weave_x(first, 0, 0, HALF, on_scalar, 0, guest("xg_a", [P, PACK * HALF], BF16, ("c512", 2112)))
+        weave_x(first, 0, 0, HALF, on_scalar, 0, guest("xg_a", [P, PACK * HALF], BF16, ("c512", 3136)))
         quantise_x(0, 0, ("plane4", 0))
         left2 = leftover_on_tensor(2)
         xg_b = guest("xg_b", [P, PACK * HALF], BF16, ("c512", 64 - 4096))
@@ -449,7 +450,8 @@ def tile_list_noneP_kernel(
         quantise_part(5, 5, 1)
         round_copied_y(6, 6)
         round_y(6, 7)
-        quantise_part(6, 6, 2)
+        quantise_part(6, 6, 1)
+        quantise_part(6, 7, 1)
         store_words(5, 3)
 
         for q in range(4):

@@ -55,10 +55,10 @@ def tile_list_noneP_kernel(
         shared = ctx.enter_context(tc.tile_pool(name="shared", bufs=1))
         starts = {}
 
-        def host(name, shape, before=0, spare=0):
+        def host(name, shape, before=0, spare=0, dtype=F32):
             starts[name] = starts.get("end", 0) + before
             starts["end"] = starts[name] + 4 * math.prod(shape[1:]) + spare
-            return shared.tile(shape, F32, name=name, offset=starts[name], align_bytes=64)
+            return shared.tile(shape, dtype, name=name, offset=starts[name], align_bytes=64)
 
         def guest(name, shape, dtype, slot):
             if slot is None:
@@ -78,13 +78,14 @@ def tile_list_noneP_kernel(
         nc.sync.dma_start(wx_raw[:].bitcast(I32), wx_words[0].bitcast(I32))
         wt_raw = keep.tile([P, 2, N], I32, name="wt_raw", align_bytes=64)
 
-        scales_raw = keep.tile([P, N], U8, name="scales_raw", align_bytes=64)
-        nc.vector.memset(scales_raw[:].bitcast(I32), 0)
+        scales_words = host("scales_raw", [P, N // 4], 1024, 4096, I32)
+        scales_raw = scales_words[:].bitcast(U8)
+        nc.vector.memset(scales_words[:], 0)
 
         square = keep.tile([P, P], F32, name="square")
         ones = keep.tile([P, P], F32, name="ones")
         nc.vector.memset(ones[:], 1.0)
-        column = keep.tile([P, P], F32, name="column", align_bytes=64)
+        column = host("column", [P, P], 0, 4096)
         nc.vector.tensor_tensor_scan(column[:], ones[:], ones[:], -1.0, MULT, ADD)
         in_group = keep.tile([P, 32], F32, name="in_group", align_bytes=64)
         nc.vector.transpose(in_group[:], column[:, :32])
@@ -92,17 +93,17 @@ def tile_list_noneP_kernel(
         for q in range(4):
             nc.vector.memset(group_start[32 * q : 32 * (q + 1), :], 32.0 * q)
         nc.vector.tensor_scalar(square[:], column[:], group_start[:], in_group[:, 0:1], SUB, EQUAL)
-        eye = keep.tile([P, PACK * P * PACK], BF16, name="eye", align_bytes=64)
+        eye = guest("eye", [P, PACK * P * PACK], BF16, ("column", 0))
         nc.vector.memset(eye[:].bitcast(I32), 0)
         for t in range(PACK):
             nc.vector.tensor_copy(eye[:, PACK * P * t + t : PACK * P * (t + 1) : PACK], square[:])
 
         def load_scales(q):
             nc.sync.dma_start(
-                scales_raw[32 * q : 32 * q + 4, :].bitcast(I32), wx_scales[0, 4 * q : 4 * q + 4, :].bitcast(I32)
+                scales_words[32 * q : 32 * q + 4, :], wx_scales[0, 4 * q : 4 * q + 4, :].bitcast(I32)
             )
             nc.sync.dma_start(
-                scales_raw[32 * q + 4 : 32 * q + 12, :].bitcast(I32), wt_scales[:, 4 * q : 4 * q + 4, :].bitcast(I32)
+                scales_words[32 * q + 4 : 32 * q + 12, :], wt_scales[:, 4 * q : 4 * q + 4, :].bitcast(I32)
             )
 
         w_sb = keep.tile([P, J], F32, name="w_sb")
@@ -164,7 +165,7 @@ def tile_list_noneP_kernel(
         scales_dealt = keep.tile([P, N], U8, name="scales_dealt", align_bytes=64)
         nc.vector.tensor_copy(
             scales_dealt[:].rearrange("p (t g m) -> p g t m", t=PACK, m=16),
-            scales_raw[:].rearrange("p (g m t) -> p g t m", t=PACK, m=16),
+            scales_raw.rearrange("p (g m t) -> p g t m", t=PACK, m=16),
         )
 
         xq = ({}, {})
@@ -369,7 +370,9 @@ def tile_list_noneP_kernel(
         late = gathered.tile([P, PACK * (J - LATE)], F32, name="late", align_bytes=64)
         middle_rows = middle[:].rearrange("p (t j) -> p t j", t=PACK)
         late_rows = late[:].rearrange("p (t j) -> p t j", t=PACK)
-        for u in range(PACK):
+        gather(first, 0, 0, HALF)
+        gather(first, 0, HALF, HALF)
+        for u in range(1, PACK):
             gather(first, u, 0, J)
         for u in (4, 5):
             gather(early, u, 0, EARLY)
@@ -381,12 +384,12 @@ def tile_list_noneP_kernel(
         left0 = leftover_on_tensor(0, ("c256", 0))
         weave_c(1)
         first_tier(1)
-        second_tier(0, left0, CHUNK, ("c512", 2112))
+        second_tier(0, left0, CHUNK, ("scales_raw", 64 - 1024))
         left1 = leftover_on_tensor(1, ("c512", 64))
         weave_c(2)
         first_tier(2)
         second_tier(CHUNK, left1, CHUNK, ("plane4", 2048))
-        weave_x(first, 0, 0, HALF, on_scalar, 0, guest("xg_a", [P, PACK * HALF], BF16, ("c512", 3136)))
+        weave_x(first, 0, 0, HALF, on_scalar, 0, guest("xg_a", [P, PACK * HALF], BF16, ("scales_raw", 64)))
         quantise_x(0, 0, ("plane4", 0))
         left2 = leftover_on_tensor(2)
         xg_b = guest("xg_b", [P, PACK * HALF], BF16, ("c512", 64 - 4096))
@@ -447,8 +450,8 @@ def tile_list_noneP_kernel(
         round_copied_y(5, 5)
         quantise_part(0, 0, 2)
         store_words(0, 2)
-        quantise_part(5, 5, 1)
         round_copied_y(6, 6)
+        quantise_part(5, 5, 1)
         round_y(6, 7)
         quantise_part(6, 6, 1)
         quantise_part(6, 7, 1)

@@ -21,17 +21,28 @@ EQUAL = mybir.AluOpType.is_equal
 COPY = mybir.ActivationFunctionType.Copy
 
 P = 128
+QUADRANT = 32
 PACK = 4
+HEADS = 8
 LIST_ROWS = 16
-BLOCK = 128
+STRIP = 128
 CHUNK = 256
 HALF = 512
 RUN = 4
+EDGE = 64
+
+MIDDLE = 3 * STRIP
+LATE = 5 * STRIP
+LAST = 7 * STRIP
 
 VALUE_BANKS = (4, 5)
 TURN_BANKS = ((6, 7), (0, 1))
 TURN_BACK_BANK = 3
 Y_BANKS = (0, 1, 2, 3, 6, 7, 0, 1)
+
+FIRST_TIER, SECOND_TIER, PASS_0, PASS_1 = range(4)
+
+Y_GROUPS = ((0, 2), (2, 3), (5, 1), (6, 2))
 
 
 def woven(ap):
@@ -48,77 +59,74 @@ def tile_list_noneP_kernel(
     nc = tc.nc
     with ExitStack() as ctx:
         keep = ctx.enter_context(tc.tile_pool(name="keep", bufs=1))
-        gathered = ctx.enter_context(tc.tile_pool(name="gathered", bufs=1))
         psum = ctx.enter_context(tc.psum_pool(name="psum", bufs=1))
         stage = ctx.enter_context(tc.tile_pool(name="stage", bufs=2))
-
         shared = ctx.enter_context(tc.tile_pool(name="shared", bufs=1))
-        starts = {}
+        start_of = {"free": 0}
 
-        def host(name, shape, before=0, spare=0, dtype=F32):
-            starts[name] = starts.get("end", 0) + before
-            starts["end"] = starts[name] + 4 * math.prod(shape[1:]) + spare
-            return shared.tile(shape, dtype, name=name, offset=starts[name], align_bytes=64)
+        def host(name, shape, dtype=F32, before=0, behind=0):
+            start_of[name] = start_of["free"] + before
+            start_of["free"] = start_of[name] + 4 * math.prod(shape[1:]) + behind
+            return shared.tile(shape, dtype, name=name, offset=start_of[name], align_bytes=64)
 
-        def guest(name, shape, dtype, slot):
-            if slot is None:
+        def tile_at(name, shape, dtype, place=None):
+            if place is None:
                 return keep.tile(shape, dtype, name=name, align_bytes=64)
-            return shared.tile(shape, dtype, name=name, offset=starts[slot[0]] + slot[1], align_bytes=64)
+            return shared.tile(shape, dtype, name=name, offset=start_of[place[0]] + place[1], align_bytes=64)
 
         offsets = keep.tile([P, J // LIST_ROWS], U16, name="offsets")
         nc.sync.dma_start(offsets[:], offs)
 
         w_rows = keep.tile([P, P], F32, name="w_rows")
         nc.sync.dma_start(
-            w_rows[:], wgt.rearrange("(g r) j -> g (r j)", r=LIST_ROWS)[:, : 2 * J].rearrange("g (q c) -> g q c", c=P)
+            w_rows[:], wgt.rearrange("(g r) j -> g (r j)", r=LIST_ROWS)[:, : 2 * J].rearrange("g (q m) -> g q m", m=P)
         )
-        c_first = host("c0", [P, PACK, CHUNK])
-        nc.sync.dma_start(c_first[:], c.rearrange("(p t) j -> p t j", t=PACK)[:, :, :CHUNK])
+
+        woven_half = 2 * PACK * HALF
+        c_sb = [
+            host("c%d" % part, [P, PACK, CHUNK], before=woven_half if part == 2 else 0) for part in range(J // CHUNK)
+        ]
+        c_rows = c.rearrange("(p t) j -> p t j", t=PACK)
+
+        def load_c(part):
+            nc.sync.dma_start(c_sb[part][:], c_rows[:, :, part * CHUNK : (part + 1) * CHUNK])
+
+        load_c(0)
         wx_raw = keep.tile([P, 2 * N], U8, name="wx_raw", align_bytes=64)
         nc.sync.dma_start(wx_raw[:].bitcast(I32), wx_words[0].bitcast(I32))
-        wt_raw = keep.tile([P, 2, N], I32, name="wt_raw", align_bytes=64)
 
-        scales_words = host("scales_raw", [P, N // 4], 1024, 4096, I32)
-        scales_raw = scales_words[:].bitcast(U8)
-        nc.vector.memset(scales_words[:], 0)
+        chunk_codes = 4 * CHUNK
+        scales_raw = host("scales_raw", [P, N // 4], I32, before=chunk_codes, behind=woven_half)
+        nc.vector.memset(scales_raw[:], 0)
 
         square = keep.tile([P, P], F32, name="square")
         ones = keep.tile([P, P], F32, name="ones")
         nc.vector.memset(ones[:], 1.0)
-        column = host("column", [P, P], 0, 4096)
+        column = host("column", [P, P], behind=2 * PACK * P * PACK)
         nc.vector.tensor_tensor_scan(column[:], ones[:], ones[:], -1.0, MULT, ADD)
-        in_group = keep.tile([P, 32], F32, name="in_group", align_bytes=64)
-        nc.vector.transpose(in_group[:], column[:, :32])
-        group_start = keep.tile([P, 1], F32, name="group_start")
-        for q in range(4):
-            nc.vector.memset(group_start[32 * q : 32 * (q + 1), :], 32.0 * q)
-        nc.vector.tensor_scalar(square[:], column[:], group_start[:], in_group[:, 0:1], SUB, EQUAL)
-        eye = guest("eye", [P, PACK * P * PACK], BF16, ("column", 0))
+        in_quadrant = keep.tile([P, QUADRANT], F32, name="in_quadrant", align_bytes=64)
+        nc.vector.transpose(in_quadrant[:], column[:, :QUADRANT])
+        quadrant_start = keep.tile([P, 1], F32, name="quadrant_start")
+        for p0 in range(0, P, QUADRANT):
+            nc.vector.memset(quadrant_start[p0 : p0 + QUADRANT, :], float(p0))
+        nc.vector.tensor_scalar(square[:], column[:], quadrant_start[:], in_quadrant[:, 0:1], SUB, EQUAL)
+
+        eye = tile_at("eye", [P, PACK * P * PACK], BF16, ("column", 0))
         nc.vector.memset(eye[:].bitcast(I32), 0)
         for t in range(PACK):
             nc.vector.tensor_copy(eye[:, PACK * P * t + t : PACK * P * (t + 1) : PACK], square[:])
 
-        def load_scales(q):
-            nc.sync.dma_start(
-                scales_words[32 * q : 32 * q + 4, :], wx_scales[0, 4 * q : 4 * q + 4, :].bitcast(I32)
-            )
-            nc.sync.dma_start(
-                scales_words[32 * q + 4 : 32 * q + 12, :], wt_scales[:, 4 * q : 4 * q + 4, :].bitcast(I32)
-            )
-
-        w_sb = keep.tile([P, J], F32, name="w_sb")
         planes = [host("plane%d" % u, [P, T]) for u in range(2 * PACK)]
-        c_parts = tuple((j0, CHUNK) for j0 in range(0, J, CHUNK))
-        c_sb = [c_first] + [host("c%d" % j0, [P, PACK, width], 4096, 4096) for j0, width in c_parts[1:]]
         x_rows = xT.rearrange("(a p t) s -> a t p s", a=2, t=PACK)
-        c_rows = c.rearrange("(p t) j -> p t j", t=PACK)
+        wt_raw = keep.tile([P, 2, N], I32, name="wt_raw", align_bytes=64)
 
         def load_plane(u):
             nc.sync.dma_start(planes[u][:], x_rows[u // PACK, u % PACK])
 
-        def load_c(part):
-            j0, width = c_parts[part]
-            nc.sync.dma_start(c_sb[part][:], c_rows[:, :, j0 : j0 + width])
+        def load_scales(q):
+            p0 = QUADRANT * q
+            nc.sync.dma_start(scales_raw[p0 : p0 + 4, :], wx_scales[0, 4 * q : 4 * q + 4, :].bitcast(I32))
+            nc.sync.dma_start(scales_raw[p0 + 4 : p0 + 12, :], wt_scales[:, 4 * q : 4 * q + 4, :].bitcast(I32))
 
         load_plane(0)
         load_plane(1)
@@ -132,16 +140,20 @@ def tile_list_noneP_kernel(
         load_scales(3)
         load_plane(4)
         nc.sync.dma_start(wt_raw[:], wt_words.rearrange("a p n i -> p a (n i)").bitcast(I32))
-        for u in range(5, 8):
+        for u in range(5, 2 * PACK):
             load_plane(u)
         load_c(3)
 
+        w_sb = keep.tile([P, J], F32, name="w_sb")
         w_turned = psum.tile([P, P], F32, name="w_turned", tag="bank2")
         nc.tensor.transpose(w_turned[:], w_rows[:], square[:])
         w_wide = keep.tile([P, J], F32, name="w_wide")
         nc.scalar.copy(
-            w_wide[:].rearrange("c (b g i) -> c b g i", g=8, i=LIST_ROWS),
-            w_turned[:].rearrange("c (g q) -> c q g", q=LIST_ROWS)[:, :8, :].unsqueeze(3).to_broadcast([P, 8, 8, LIST_ROWS]),
+            w_wide[:].rearrange("m (q g i) -> m q g i", g=HEADS, i=LIST_ROWS),
+            w_turned[:]
+            .rearrange("m (g q) -> m q g", q=LIST_ROWS)[:, : J // P, :]
+            .unsqueeze(3)
+            .to_broadcast([P, J // P, HEADS, LIST_ROWS]),
         )
         for h in range(2):
             w_back = psum.tile([P, HALF], F32, name="w_back", tag="bank%d" % h)
@@ -165,21 +177,19 @@ def tile_list_noneP_kernel(
         scales_dealt = keep.tile([P, N], U8, name="scales_dealt", align_bytes=64)
         nc.vector.tensor_copy(
             scales_dealt[:].rearrange("p (t g m) -> p g t m", t=PACK, m=16),
-            scales_raw.rearrange("p (g m t) -> p g t m", t=PACK, m=16),
+            scales_raw[:].bitcast(U8).rearrange("p (g m t) -> p g t m", t=PACK, m=16),
         )
 
-        xq = ({}, {})
-        cq = {}
-        cr = {}
+        moving = ({}, {}, {}, {})
 
-        def quantise(into, name, src, j0, width, slot=None):
-            codes = guest(name + "_codes", [P, width], U32, slot)
-            scales = keep.tile([P, width], U8, name=name + "_scales", align_bytes=64)
-            nc.vector.quantize_mx(out=codes[:].bitcast(FP8X4), scales=scales[:], in_=src)
-            for s in range(0, width, BLOCK):
-                into[j0 + s] = (codes[:, s : s + BLOCK], scales[:, s : s + BLOCK])
+        def quantise(term, src, j0, width, place=None):
+            codes = tile_at("codes%d_%d" % (term, j0), [P, width], U32, place)
+            scales = tile_at("scales%d_%d" % (term, j0), [P, width], U8)
+            nc.vector.quantize_mx(out=codes[:].bitcast(FP8X4), scales=scales[:], in_=src[:])
+            for s in range(0, width, STRIP):
+                moving[term][j0 + s] = (codes[:, s : s + STRIP], scales[:, s : s + STRIP])
 
-        def gather(picked, u, j0, width, base=0):
+        def gather(picked, base, u, j0, width):
             nc.vector.tensor_tensor(
                 picked[:, u % PACK, j0 - base : j0 - base + width],
                 planes[u][:].indirect(offsets[:, j0 // LIST_ROWS : (j0 + width) // LIST_ROWS]),
@@ -187,31 +197,16 @@ def tile_list_noneP_kernel(
                 MULT,
             )
 
-        xg = {}
-        cb = {}
+        def weave(copy, rounded, source, s, width):
+            copy(woven(rounded[:]), by_rows(source[:, :, s : s + width]))
+            return rounded
 
-        def weave_x(picked, a, j0, width, copy, base=0, into=None):
-            if into is None:
-                into = keep.tile([P, PACK * width], BF16, name="xg", tag="xg%d_%d" % (a, j0), align_bytes=64)
-            rounded = into
-            copy(woven(rounded[:]), by_rows(picked[:, :, j0 - base : j0 - base + width]))
-            xg[a, j0] = (rounded, width)
-
-        def quantise_x(a, j0, codes_slot=None):
-            rounded, width = xg[a, j0]
-            quantise(xq[a], "xq%d_%d" % (a, j0), rounded[:], j0, width, codes_slot)
-
-        def weave_c(part, slot=None):
-            rounded = guest("cb%d" % part, [P, PACK * CHUNK], BF16, slot)
-            nc.scalar.copy(woven(rounded[:]), by_rows(c_sb[part][:]))
-            cb[part] = rounded
-
-        def first_tier(part, codes_slot=None):
-            quantise(cq, "cq%d" % part, cb[part][:], part * CHUNK, CHUNK, codes_slot)
+        def weave_c(part):
+            return weave(nc.scalar.copy, tile_at("c_woven%d" % part, [P, PACK * CHUNK], BF16), c_sb[part], 0, CHUNK)
 
         def values_of(j):
-            codes, scales = cq[j]
-            values = psum.tile([P, PACK, BLOCK], F32, name="values", tag="bank%d" % VALUE_BANKS[j // BLOCK % 2])
+            codes, scales = moving[FIRST_TIER][j]
+            values = psum.tile([P, PACK, STRIP], F32, name="values", tag="bank%d" % VALUE_BANKS[j // STRIP % 2])
             for t in range(PACK):
                 nc.tensor.matmul_mx(
                     out=values[:, t, :],
@@ -224,33 +219,33 @@ def tile_list_noneP_kernel(
                 )
             return values
 
-        def leftover_on_vector(part, s0):
-            left = keep.tile([P, PACK * CHUNK], BF16, name="left%d_%d" % (part, s0), align_bytes=64)
-            for s in range(0, CHUNK, BLOCK):
+        def leftover_on_vector(part):
+            left = tile_at("left%d" % part, [P, PACK * CHUNK], BF16)
+            for s in range(0, CHUNK, STRIP):
                 nc.vector.tensor_tensor(
-                    woven(left[:, PACK * s : PACK * (s + BLOCK)]),
-                    by_rows(c_sb[part][:, :, s0 + s : s0 + s + BLOCK]),
-                    by_rows(values_of(c_parts[part][0] + s0 + s)[:]),
+                    woven(left[:, PACK * s : PACK * (s + STRIP)]),
+                    by_rows(c_sb[part][:, :, s : s + STRIP]),
+                    by_rows(values_of(part * CHUNK + s)[:]),
                     SUB,
                 )
             return left
 
-        def leftover_on_tensor(part, slot=None):
-            left = guest("left%d" % part, [P, PACK * CHUNK], BF16, slot)
-            turned_back = psum.tile([P, 2, 2, BLOCK], F32, name="turned_back", tag="bank%d" % TURN_BACK_BANK)
-            for b in range(CHUNK // BLOCK):
-                s = b * BLOCK
-                negated = stage.tile([P, PACK, BLOCK], F32, name="negated")
-                nc.scalar.activation(negated[:], values_of(c_parts[part][0] + s)[:], COPY, scale=-1.0)
+        def leftover_on_tensor(part, place=None):
+            left = tile_at("left%d" % part, [P, PACK * CHUNK], BF16, place)
+            turned_back = psum.tile([P, 2, 2, STRIP], F32, name="turned_back", tag="bank%d" % TURN_BACK_BANK)
+            for b in range(CHUNK // STRIP):
+                s = b * STRIP
+                negated = stage.tile([P, PACK, STRIP], F32, name="negated")
+                nc.scalar.activation(negated[:], values_of(part * CHUNK + s)[:], COPY, scale=-1.0)
                 turned = psum.tile([P, PACK, P], F32, name="turned", tag="bank%d" % TURN_BANKS[part % 2][b])
-                for term, (source, col) in enumerate(((c_sb[part][:], s), (negated[:], 0))):
+                for second, (source, col) in enumerate(((c_sb[part], s), (negated, 0))):
                     for t in range(PACK):
                         nc.tensor.matmul(
                             turned[:, t, :],
-                            source[:, t, col : col + BLOCK],
+                            source[:, t, col : col + STRIP],
                             square[:],
-                            start=(term == 0 and t == 0),
-                            stop=(term == 1 and t == PACK - 1),
+                            start=(not second and t == 0),
+                            stop=(second == 1 and t == PACK - 1),
                             is_transpose=True,
                         )
                 pairs = stage.tile([P, PACK * P], BF16, name="pairs")
@@ -266,199 +261,160 @@ def tile_list_noneP_kernel(
             )
             return left
 
-        def second_tier(j0, left, width, codes_slot=None):
-            for s in range(0, CHUNK, width):
-                quantise(cr, "cr%d" % (j0 + s), left[:, PACK * s : PACK * (s + width)], j0 + s, width, codes_slot)
-
-        y_codes = keep.tile([P, J], U32, name="y_codes", align_bytes=64)
-        y_scales = keep.tile([P, J], U8, name="y_scales", align_bytes=64)
-        y_rows = out_0.rearrange("(p t) j -> p t j", t=PACK)
-        words_out = out_1[0].rearrange("p j i -> p (j i)").bitcast(I32)
-
         sums = {}
-        done = {}
+        terms_left = {}
 
         def add_terms(b, terms):
-            j = b * BLOCK
-            if b not in sums:
-                sums[b] = psum.tile([P, PACK, BLOCK], F32, name="acc", tag="bank%d" % Y_BANKS[b])
-                done[b] = []
+            if FIRST_TIER in terms:
+                sums[b] = psum.tile([P, PACK, STRIP], F32, name="sum", tag="bank%d" % Y_BANKS[b])
+                terms_left[b] = len(moving)
             for term in terms:
-                done[b].append(term)
-                codes, scales = (cq, cr, xq[0], xq[1])[term][j]
+                terms_left[b] = terms_left[b] - 1
+                codes, scales = moving[term][b * STRIP]
                 for t in range(PACK):
                     cols = slice(t * P, (t + 1) * P)
-                    if term < 2:
+                    if term in (FIRST_TIER, SECOND_TIER):
                         weights = wx_dealt[:, 2 * t * P : 2 * (t + 1) * P].bitcast(FP4X4)
                         weight_scales = scales_dealt[:, cols]
                     else:
-                        weights = wt_dealt[:, term - 2, cols].bitcast(FP8X4)
-                        weight_scales = scales_dealt[4 * (term - 1) : P, cols]
+                        a = term - PASS_0
+                        weights = wt_dealt[:, a, cols].bitcast(FP8X4)
+                        weight_scales = scales_dealt[4 * (a + 1) : P, cols]
                     nc.tensor.matmul_mx(
                         out=sums[b][:, t, :],
                         lhsT=weights,
                         lhsT_scale=weight_scales,
                         rhs=codes.bitcast(FP8X4),
                         rhs_scale=scales,
-                        start=(term == 0 and t == 0),
-                        stop=(len(done[b]) == 4 and t == PACK - 1),
+                        start=(term == FIRST_TIER and t == 0),
+                        stop=(terms_left[b] == 0 and t == PACK - 1),
                     )
 
-        y_rounded = {}
+        first = keep.tile([P, PACK, J], F32, name="first")
+        early = host("early", [P, PACK, MIDDLE])
+        middle_row = keep.tile([P, PACK * (LATE - MIDDLE)], F32, name="middle", align_bytes=64)
+        late_row = keep.tile([P, PACK * (J - LATE)], F32, name="late", align_bytes=64)
+        middle = middle_row[:].rearrange("p (t j) -> p t j", t=PACK)
+        late = late_row[:].rearrange("p (t j) -> p t j", t=PACK)
+        gather(first, 0, 0, 0, HALF)
+        gather(first, 0, 0, HALF, HALF)
+        for u in range(1, PACK):
+            gather(first, 0, u, 0, J)
+        for u in (4, 5):
+            gather(early, 0, u, 0, MIDDLE)
+            gather(middle, MIDDLE, u, MIDDLE, LATE - MIDDLE)
+            gather(late, LATE, u, LATE, J - LATE)
+        gather(early, 0, 6, 0, MIDDLE)
 
-        y_float = {}
+        quantise(FIRST_TIER, weave_c(0), 0, CHUNK)
+        left_0 = leftover_on_tensor(0, ("c1", 0))
+        quantise(FIRST_TIER, weave_c(1), CHUNK, CHUNK)
+        quantise(SECOND_TIER, left_0, 0, CHUNK, ("scales_raw", EDGE - chunk_codes))
+        left_1 = leftover_on_tensor(1, ("c2", EDGE))
+        quantise(FIRST_TIER, weave_c(2), 2 * CHUNK, CHUNK)
+        quantise(SECOND_TIER, left_1, CHUNK, CHUNK, ("plane4", 2 * chunk_codes))
+        half_0 = tile_at("half_0", [P, PACK * HALF], BF16, ("scales_raw", EDGE))
+        quantise(PASS_0, weave(nc.scalar.copy, half_0, first, 0, HALF), 0, HALF, ("plane4", 0))
+        left_2 = leftover_on_tensor(2)
+        half_1 = tile_at("half_1", [P, PACK * HALF], BF16, ("c2", EDGE - woven_half))
+        for s in (0, CHUNK):
+            weave(nc.scalar.copy, half_1[:, PACK * s : PACK * (s + CHUNK)], first, HALF + s, CHUNK)
+        for b in range(HALF // STRIP):
+            add_terms(b, (FIRST_TIER, SECOND_TIER, PASS_0))
 
-        def open_y(b0, blocks):
-            y_float[b0] = keep.tile([P, PACK, BLOCK * blocks], F32, name="y%d" % b0)
-            y_rounded[b0] = (keep.tile([P, PACK * BLOCK * blocks], BF16, name="yb%d" % b0, align_bytes=64), BLOCK * blocks)
+        gather(early, 0, 7, 0, STRIP)
+        gather(early, 0, 7, STRIP, CHUNK)
+        strip_0 = weave(nc.scalar.copy, middle_row[:, 2 * CHUNK : 3 * CHUNK].bitcast(BF16), early, 0, STRIP)
+        strips_1_2 = weave(nc.scalar.copy, late_row[:, 4 * CHUNK : 6 * CHUNK].bitcast(BF16), early, STRIP, CHUNK)
+        quantise(PASS_1, strip_0, 0, STRIP)
+        add_terms(0, (PASS_1,))
+        gather(middle, MIDDLE, 6, MIDDLE, LATE - MIDDLE)
+        gather(middle, MIDDLE, 7, MIDDLE, LATE - MIDDLE)
+        quantise(PASS_1, strips_1_2, STRIP, CHUNK)
+        add_terms(1, (PASS_1,))
+        add_terms(2, (PASS_1,))
 
-        def copy_y(b0, b, copy):
-            s = (b - b0) * BLOCK
-            copy(y_float[b0][:, :, s : s + BLOCK], sums[b][:])
+        c_woven_3 = weave_c(3)
+        strips_3_4 = weave(nc.scalar.copy, tile_at("strips_3_4", [P, PACK * CHUNK], BF16), middle, 0, CHUNK)
+        quantise(PASS_0, half_1, HALF, HALF, ("early", 0))
+        quantise(SECOND_TIER, left_2, 2 * CHUNK, CHUNK, ("early", 2 * chunk_codes))
+        gather(late, LATE, 6, LATE, J - LATE)
+        quantise(PASS_1, strips_3_4, MIDDLE, CHUNK)
+        add_terms(3, (PASS_1,))
+        add_terms(4, (FIRST_TIER, PASS_0, SECOND_TIER, PASS_1))
+        quantise(FIRST_TIER, c_woven_3, 3 * CHUNK, CHUNK)
+        gather(late, LATE, 7, LATE, J - LATE)
+        strips_5_6 = weave(nc.vector.tensor_copy, tile_at("strips_5_6", [P, PACK * CHUNK], BF16), late, 0, CHUNK)
+        left_3 = leftover_on_vector(3)
+        quantise(PASS_1, strips_5_6, LATE, CHUNK)
+        add_terms(5, (FIRST_TIER, PASS_0, SECOND_TIER, PASS_1))
+        strip_7 = weave(nc.vector.tensor_copy, tile_at("strip_7", [P, PACK * STRIP], BF16), late, LAST - LATE, STRIP)
+        quantise(SECOND_TIER, left_3, 3 * CHUNK, CHUNK)
+        quantise(PASS_1, strip_7, LAST, STRIP)
 
-        def round_y(b0, b):
-            s = (b - b0) * BLOCK
-            nc.scalar.copy(
-                y_rounded[b0][0][:, PACK * s : PACK * (s + BLOCK)].rearrange("p (j t) -> p j t", t=PACK),
-                sums[b][:].rearrange("p t j -> p j t"),
-            )
+        y_codes = keep.tile([P, J], U32, name="y_codes", align_bytes=64)
+        y_scales = keep.tile([P, J], U8, name="y_scales", align_bytes=64)
+        y_rows = out_0.rearrange("(p t) j -> p t j", t=PACK)
+        words_out = out_1[0].rearrange("p j i -> p (j i)").bitcast(I32)
+        y_group = {}
+        for b0, strips in Y_GROUPS:
+            y_float = keep.tile([P, PACK, strips * STRIP], F32, name="y_float%d" % b0)
+            y_woven = tile_at("y_woven%d" % b0, [P, PACK * strips * STRIP], BF16)
+            for b in range(b0, b0 + strips):
+                y_group[b] = (b0, strips, y_float, y_woven)
 
-        def round_copied_y(b0, b, blocks=1):
-            s = (b - b0) * BLOCK
-            width = BLOCK * blocks
-            nc.vector.tensor_copy(
-                woven(y_rounded[b0][0][:, PACK * s : PACK * (s + width)]), by_rows(y_float[b0][:, :, s : s + width])
-            )
+        def woven_part(b, strips):
+            b0, y_woven = y_group[b][0], y_group[b][3]
+            return y_woven[:, PACK * (b - b0) * STRIP : PACK * (b - b0 + strips) * STRIP]
 
-        def store_y(b0):
-            width = y_rounded[b0][1]
-            nc.sync.dma_start(y_rows[:, :, b0 * BLOCK : b0 * BLOCK + width], y_float[b0][:])
+        def copy_out(b):
+            b0, strips, y_float = y_group[b][:3]
+            nc.scalar.copy(y_float[:, :, (b - b0) * STRIP : (b - b0 + 1) * STRIP], sums[b][:])
+            if b == b0 + strips - 1:
+                nc.sync.dma_start(y_rows[:, :, b0 * STRIP : (b0 + strips) * STRIP], y_float[:])
 
-        def drain(b0, blocks):
-            open_y(b0, blocks)
-            for b in range(b0, b0 + blocks):
-                copy_y(b0, b, nc.scalar.copy)
-            store_y(b0)
-            for b in range(b0, b0 + blocks):
-                round_y(b0, b)
+        def round_from_bank(b):
+            nc.scalar.copy(woven_part(b, 1).rearrange("p (j t) -> p j t", t=PACK), sums[b][:].rearrange("p t j -> p j t"))
 
-        def quantise_y(b0):
-            rounded, width = y_rounded[b0]
-            cols = slice(b0 * BLOCK, b0 * BLOCK + width)
-            nc.vector.quantize_mx(out=y_codes[:, cols].bitcast(FP8X4), scales=y_scales[:, cols], in_=rounded[:])
+        def round_from_copy(b, strips):
+            b0, y_float = y_group[b][0], y_group[b][2]
+            weave(nc.vector.tensor_copy, woven_part(b, strips), y_float, (b - b0) * STRIP, strips * STRIP)
 
-        def quantise_part(b0, b, blocks):
-            s = PACK * (b - b0) * BLOCK
-            cols = slice(b * BLOCK, (b + blocks) * BLOCK)
+        def quantise_y(b, strips):
+            cols = slice(b * STRIP, (b + strips) * STRIP)
             nc.vector.quantize_mx(
-                out=y_codes[:, cols].bitcast(FP8X4),
-                scales=y_scales[:, cols],
-                in_=y_rounded[b0][0][:, s : s + PACK * blocks * BLOCK],
+                out=y_codes[:, cols].bitcast(FP8X4), scales=y_scales[:, cols], in_=woven_part(b, strips)
             )
 
-        def store_words(b0, blocks):
-            cols = slice(b0 * BLOCK, (b0 + blocks) * BLOCK)
+        def store_words(b, strips):
+            cols = slice(b * STRIP, (b + strips) * STRIP)
             nc.sync.dma_start(words_out[:, cols], y_codes[:, cols].bitcast(I32))
 
-        on_scalar, on_vector = nc.scalar.copy, nc.vector.tensor_copy
-
-        EARLY = 3 * BLOCK
-        LATE = 5 * BLOCK
-        first = gathered.tile([P, PACK, J], F32, name="first")
-        early = host("early", [P, PACK, EARLY])
-        middle = gathered.tile([P, PACK * CHUNK], F32, name="middle", align_bytes=64)
-        late = gathered.tile([P, PACK * (J - LATE)], F32, name="late", align_bytes=64)
-        middle_rows = middle[:].rearrange("p (t j) -> p t j", t=PACK)
-        late_rows = late[:].rearrange("p (t j) -> p t j", t=PACK)
-        gather(first, 0, 0, HALF)
-        gather(first, 0, HALF, HALF)
-        for u in range(1, PACK):
-            gather(first, u, 0, J)
-        for u in (4, 5):
-            gather(early, u, 0, EARLY)
-            gather(middle_rows, u, EARLY, CHUNK, EARLY)
-            gather(late_rows, u, LATE, J - LATE, LATE)
-        gather(early, 6, 0, EARLY)
-        weave_c(0)
-        first_tier(0)
-        left0 = leftover_on_tensor(0, ("c256", 0))
-        weave_c(1)
-        first_tier(1)
-        second_tier(0, left0, CHUNK, ("scales_raw", 64 - 1024))
-        left1 = leftover_on_tensor(1, ("c512", 64))
-        weave_c(2)
-        first_tier(2)
-        second_tier(CHUNK, left1, CHUNK, ("plane4", 2048))
-        weave_x(first, 0, 0, HALF, on_scalar, 0, guest("xg_a", [P, PACK * HALF], BF16, ("scales_raw", 64)))
-        quantise_x(0, 0, ("plane4", 0))
-        left2 = leftover_on_tensor(2)
-        xg_b = guest("xg_b", [P, PACK * HALF], BF16, ("c512", 64 - 4096))
-        for s in (0, CHUNK):
-            nc.scalar.copy(woven(xg_b[:, PACK * s : PACK * (s + CHUNK)]), by_rows(first[:, :, HALF + s : HALF + s + CHUNK]))
-        xg[0, HALF] = (xg_b, HALF)
-        for b in range(4):
-            add_terms(b, (0, 1, 2))
-        gather(early, 7, 0, BLOCK)
-        gather(early, 7, BLOCK, CHUNK)
-        weave_x(early, 1, 0, BLOCK, on_scalar, 0, middle[:, 2 * CHUNK : 3 * CHUNK].bitcast(BF16))
-        weave_x(early, 1, BLOCK, CHUNK, on_scalar, 0, late[:, 4 * CHUNK : 6 * CHUNK].bitcast(BF16))
-        quantise_x(1, 0)
-        add_terms(0, (3,))
-        gather(middle_rows, 6, EARLY, CHUNK, EARLY)
-        gather(middle_rows, 7, EARLY, CHUNK, EARLY)
-        quantise_x(1, BLOCK)
-        add_terms(1, (3,))
-        add_terms(2, (3,))
-        weave_c(3)
-        weave_x(middle_rows, 1, EARLY, CHUNK, on_scalar, EARLY)
-        quantise_x(0, HALF, ("early", 0))
-        second_tier(2 * CHUNK, left2, CHUNK, ("early", 2048))
-        gather(late_rows, 6, LATE, J - LATE, LATE)
-        quantise_x(1, EARLY)
-        add_terms(3, (3,))
-        add_terms(4, (0, 2, 1, 3))
-        first_tier(3)
-        gather(late_rows, 7, LATE, J - LATE, LATE)
-        weave_x(late_rows, 1, LATE, CHUNK, on_vector, LATE)
-        left3 = leftover_on_vector(3, 0)
-        quantise_x(1, LATE)
-        add_terms(5, (0, 2, 1, 3))
-        weave_x(late_rows, 1, 7 * BLOCK, BLOCK, on_vector, LATE)
-        second_tier(3 * CHUNK, left3, CHUNK)
-        quantise_x(1, 7 * BLOCK)
-        open_y(0, 2)
-        open_y(2, 3)
-        open_y(5, 1)
-        open_y(6, 2)
         for b in range(5):
-            copy_y(0 if b < 2 else 2, b, on_scalar)
-            if b in (1, 4):
-                store_y(0 if b < 2 else 2)
+            copy_out(b)
         for b in range(2, 5):
-            round_y(2, b)
-        add_terms(6, (0, 2, 3, 1))
-        add_terms(7, (0, 2, 1, 3))
-        quantise_part(2, 2, 2)
-        quantise_part(2, 4, 1)
+            round_from_bank(b)
+        add_terms(6, (FIRST_TIER, PASS_0, PASS_1, SECOND_TIER))
+        add_terms(7, (FIRST_TIER, PASS_0, SECOND_TIER, PASS_1))
+        quantise_y(2, 2)
+        quantise_y(4, 1)
         store_words(2, 3)
-        copy_y(5, 5, on_scalar)
-        store_y(5)
-        copy_y(6, 6, on_scalar)
-        copy_y(6, 7, on_scalar)
-        store_y(6)
-        round_copied_y(0, 0, 2)
-        round_copied_y(5, 5)
-        quantise_part(0, 0, 2)
+        for b in range(5, 8):
+            copy_out(b)
+        round_from_copy(0, 2)
+        round_from_copy(5, 1)
+        quantise_y(0, 2)
         store_words(0, 2)
-        round_copied_y(6, 6)
-        quantise_part(5, 5, 1)
-        round_y(6, 7)
-        quantise_part(6, 6, 1)
-        quantise_part(6, 7, 1)
+        round_from_copy(6, 1)
+        quantise_y(5, 1)
+        round_from_bank(7)
+        quantise_y(6, 1)
+        quantise_y(7, 1)
         store_words(5, 3)
 
         for q in range(4):
             queue = nc.scalar if q % 2 else nc.sync
             queue.dma_start(
-                out_2[0, 4 * q : 4 * q + 4, :].bitcast(I32), y_scales[32 * q : 32 * q + 4, :].bitcast(I32)
+                out_2[0, 4 * q : 4 * q + 4, :].bitcast(I32),
+                y_scales[QUADRANT * q : QUADRANT * q + 4, :].bitcast(I32),
             )

@@ -23,7 +23,6 @@ COPY = mybir.ActivationFunctionType.Copy
 P = 128
 QUADRANT = 32
 PACK = 4
-HEADS = 8
 LIST_ROWS = 16
 STRIP = 128
 CHUNK = 256
@@ -46,11 +45,11 @@ Y_GROUPS = ((0, 2), (2, 3), (5, 1), (6, 2))
 
 
 def woven(ap):
-    return ap.rearrange("p (g r t) -> p g t r", r=RUN, t=PACK)
+    return ap.rearrange("p (runs run t) -> p runs t run", run=RUN, t=PACK)
 
 
 def by_rows(ap):
-    return ap.rearrange("p t (g r) -> p g t r", r=RUN)
+    return ap.rearrange("p t (runs run) -> p runs t run", run=RUN)
 
 
 def tile_list_noneP_kernel(
@@ -77,9 +76,11 @@ def tile_list_noneP_kernel(
         offsets = keep.tile([P, J // LIST_ROWS], U16, name="offsets")
         nc.sync.dma_start(offsets[:], offs)
 
+        stretches = J // P
         w_rows = keep.tile([P, P], F32, name="w_rows")
         nc.sync.dma_start(
-            w_rows[:], wgt.rearrange("(g r) j -> g (r j)", r=LIST_ROWS)[:, : 2 * J].rearrange("g (q m) -> g q m", m=P)
+            w_rows[:],
+            wgt.rearrange("(g row) j -> g (row j)", row=LIST_ROWS)[:, : 2 * J].rearrange("g (cut m) -> g cut m", m=P),
         )
 
         woven_half = 2 * PACK * HALF
@@ -117,7 +118,7 @@ def tile_list_noneP_kernel(
             nc.vector.tensor_copy(eye[:, PACK * P * t + t : PACK * P * (t + 1) : PACK], square[:])
 
         planes = [host("plane%d" % u, [P, T]) for u in range(2 * PACK)]
-        x_rows = xT.rearrange("(a p t) s -> a t p s", a=2, t=PACK)
+        x_rows = xT.rearrange("(a p t) token -> a t p token", a=2, t=PACK)
         wt_raw = keep.tile([P, 2, N], I32, name="wt_raw", align_bytes=64)
 
         def load_plane(u):
@@ -139,7 +140,7 @@ def tile_list_noneP_kernel(
         load_c(2)
         load_scales(3)
         load_plane(4)
-        nc.sync.dma_start(wt_raw[:], wt_words.rearrange("a p n i -> p a (n i)").bitcast(I32))
+        nc.sync.dma_start(wt_raw[:], wt_words.rearrange("a p n t -> p a (n t)").bitcast(I32))
         for u in range(5, 2 * PACK):
             load_plane(u)
         load_c(3)
@@ -149,11 +150,11 @@ def tile_list_noneP_kernel(
         nc.tensor.transpose(w_turned[:], w_rows[:], square[:])
         w_wide = keep.tile([P, J], F32, name="w_wide")
         nc.scalar.copy(
-            w_wide[:].rearrange("m (q g i) -> m q g i", g=HEADS, i=LIST_ROWS),
+            w_wide[:].rearrange("m (z i again) -> m z i again", z=stretches, again=stretches),
             w_turned[:]
-            .rearrange("m (g q) -> m q g", q=LIST_ROWS)[:, : J // P, :]
+            .rearrange("m (i z) -> m z i", z=stretches)
             .unsqueeze(3)
-            .to_broadcast([P, J // P, HEADS, LIST_ROWS]),
+            .to_broadcast([P, stretches, P // stretches, stretches]),
         )
         for h in range(2):
             w_back = psum.tile([P, HALF], F32, name="w_back", tag="bank%d" % h)
@@ -163,21 +164,21 @@ def tile_list_noneP_kernel(
 
         wx_dealt = keep.tile([P, 2 * N], U8, name="wx_dealt", align_bytes=64)
         nc.vector.tensor_copy(
-            wx_dealt[:].rearrange("p (t g m b) -> p g t m b", t=PACK, m=8, b=2),
-            wx_raw[:].rearrange("p (g m t b) -> p g t m b", t=PACK, m=8, b=2),
+            wx_dealt[:].rearrange("p (t lines m byte) -> p lines t m byte", t=PACK, m=8, byte=2),
+            wx_raw[:].rearrange("p (lines m t byte) -> p lines t m byte", t=PACK, m=8, byte=2),
         )
         wt_dealt = keep.tile([P, 2, N], I32, name="wt_dealt", align_bytes=64)
         nc.vector.tensor_copy(
-            wt_dealt[:].rearrange("p a (t g m) -> p a g t m", t=PACK, m=4),
-            wt_raw[:].rearrange("p a (g m t) -> p a g t m", t=PACK, m=4),
+            wt_dealt[:].rearrange("p a (t lines m) -> p a lines t m", t=PACK, m=4),
+            wt_raw[:].rearrange("p a (lines m t) -> p a lines t m", t=PACK, m=4),
         )
         eye_codes = keep.tile([P, PACK * P], U32, name="eye_codes", align_bytes=64)
         eye_scales = keep.tile([P, PACK * P], U8, name="eye_scales", align_bytes=64)
         nc.vector.quantize_mx(out=eye_codes[:].bitcast(FP8X4), scales=eye_scales[:], in_=eye[:])
         scales_dealt = keep.tile([P, N], U8, name="scales_dealt", align_bytes=64)
         nc.vector.tensor_copy(
-            scales_dealt[:].rearrange("p (t g m) -> p g t m", t=PACK, m=16),
-            scales_raw[:].bitcast(U8).rearrange("p (g m t) -> p g t m", t=PACK, m=16),
+            scales_dealt[:].rearrange("p (t lines m) -> p lines t m", t=PACK, m=16),
+            scales_raw[:].bitcast(U8).rearrange("p (lines m t) -> p lines t m", t=PACK, m=16),
         )
 
         moving = ({}, {}, {}, {})
@@ -238,26 +239,26 @@ def tile_list_noneP_kernel(
                 negated = stage.tile([P, PACK, STRIP], F32, name="negated")
                 nc.scalar.activation(negated[:], values_of(part * CHUNK + s)[:], COPY, scale=-1.0)
                 turned = psum.tile([P, PACK, P], F32, name="turned", tag="bank%d" % TURN_BANKS[part % 2][b])
-                for second, (source, col) in enumerate(((c_sb[part], s), (negated, 0))):
+                for addend, (source, col) in enumerate(((c_sb[part], s), (negated, 0))):
                     for t in range(PACK):
                         nc.tensor.matmul(
                             turned[:, t, :],
                             source[:, t, col : col + STRIP],
                             square[:],
-                            start=(not second and t == 0),
-                            stop=(second == 1 and t == PACK - 1),
+                            start=(addend == 0 and t == 0),
+                            stop=(addend == 1 and t == PACK - 1),
                             is_transpose=True,
                         )
                 pairs = stage.tile([P, PACK * P], BF16, name="pairs")
                 nc.scalar.copy(
-                    pairs[:].rearrange("j (u p e) -> j u p e", u=2, e=2),
-                    turned[:].rearrange("j (u e) p -> j u p e", u=2),
+                    pairs[:].rearrange("j (v p e) -> j v p e", v=2, e=2),
+                    turned[:].rearrange("j (v e) p -> j v p e", v=2),
                 )
-                for u in range(2):
-                    nc.tensor.transpose(turned_back[:, b, u, :], pairs[:].bitcast(F32)[:, u * P : (u + 1) * P], square[:])
+                for v in range(2):
+                    nc.tensor.transpose(turned_back[:, b, v, :], pairs[:].bitcast(F32)[:, v * P : (v + 1) * P], square[:])
             nc.scalar.copy(
-                left[:].bitcast(F32).rearrange("p (b j u) -> p b j u", b=2, u=2),
-                turned_back[:].rearrange("p b u j -> p b j u"),
+                left[:].bitcast(F32).rearrange("p (b j v) -> p b j v", b=2, v=2),
+                turned_back[:].rearrange("p b v j -> p b j v"),
             )
             return left
 
@@ -290,16 +291,16 @@ def tile_list_noneP_kernel(
                         stop=(terms_left[b] == 0 and t == PACK - 1),
                     )
 
-        first = keep.tile([P, PACK, J], F32, name="first")
+        pass_0 = keep.tile([P, PACK, J], F32, name="pass_0")
         early = host("early", [P, PACK, MIDDLE])
         middle_row = keep.tile([P, PACK * (LATE - MIDDLE)], F32, name="middle", align_bytes=64)
         late_row = keep.tile([P, PACK * (J - LATE)], F32, name="late", align_bytes=64)
         middle = middle_row[:].rearrange("p (t j) -> p t j", t=PACK)
         late = late_row[:].rearrange("p (t j) -> p t j", t=PACK)
-        gather(first, 0, 0, 0, HALF)
-        gather(first, 0, 0, HALF, HALF)
+        gather(pass_0, 0, 0, 0, HALF)
+        gather(pass_0, 0, 0, HALF, HALF)
         for u in range(1, PACK):
-            gather(first, 0, u, 0, J)
+            gather(pass_0, 0, u, 0, J)
         for u in (4, 5):
             gather(early, 0, u, 0, MIDDLE)
             gather(middle, MIDDLE, u, MIDDLE, LATE - MIDDLE)
@@ -314,11 +315,11 @@ def tile_list_noneP_kernel(
         quantise(FIRST_TIER, weave_c(2), 2 * CHUNK, CHUNK)
         quantise(SECOND_TIER, left_1, CHUNK, CHUNK, ("plane4", 2 * chunk_codes))
         half_0 = tile_at("half_0", [P, PACK * HALF], BF16, ("scales_raw", EDGE))
-        quantise(PASS_0, weave(nc.scalar.copy, half_0, first, 0, HALF), 0, HALF, ("plane4", 0))
+        quantise(PASS_0, weave(nc.scalar.copy, half_0, pass_0, 0, HALF), 0, HALF, ("plane4", 0))
         left_2 = leftover_on_tensor(2)
         half_1 = tile_at("half_1", [P, PACK * HALF], BF16, ("c2", EDGE - woven_half))
         for s in (0, CHUNK):
-            weave(nc.scalar.copy, half_1[:, PACK * s : PACK * (s + CHUNK)], first, HALF + s, CHUNK)
+            weave(nc.scalar.copy, half_1[:, PACK * s : PACK * (s + CHUNK)], pass_0, HALF + s, CHUNK)
         for b in range(HALF // STRIP):
             add_terms(b, (FIRST_TIER, SECOND_TIER, PASS_0))
 
@@ -355,7 +356,7 @@ def tile_list_noneP_kernel(
         y_codes = keep.tile([P, J], U32, name="y_codes", align_bytes=64)
         y_scales = keep.tile([P, J], U8, name="y_scales", align_bytes=64)
         y_rows = out_0.rearrange("(p t) j -> p t j", t=PACK)
-        words_out = out_1[0].rearrange("p j i -> p (j i)").bitcast(I32)
+        words_out = out_1[0].rearrange("p j t -> p (j t)").bitcast(I32)
         y_group = {}
         for b0, strips in Y_GROUPS:
             y_float = keep.tile([P, PACK, strips * STRIP], F32, name="y_float%d" % b0)
@@ -390,16 +391,17 @@ def tile_list_noneP_kernel(
             cols = slice(b * STRIP, (b + strips) * STRIP)
             nc.sync.dma_start(words_out[:, cols], y_codes[:, cols].bitcast(I32))
 
-        for b in range(5):
+        first_late = LATE // STRIP
+        for b in range(first_late):
             copy_out(b)
-        for b in range(2, 5):
+        for b in range(2, first_late):
             round_from_bank(b)
         add_terms(6, (FIRST_TIER, PASS_0, PASS_1, SECOND_TIER))
         add_terms(7, (FIRST_TIER, PASS_0, SECOND_TIER, PASS_1))
         quantise_y(2, 2)
         quantise_y(4, 1)
         store_words(2, 3)
-        for b in range(5, 8):
+        for b in range(first_late, J // STRIP):
             copy_out(b)
         round_from_copy(0, 2)
         round_from_copy(5, 1)

@@ -169,8 +169,8 @@ def tile_list_noneP_kernel(
         )
         wt_dealt = keep.tile([P, 2, N], I32, name="wt_dealt", align_bytes=64)
         nc.vector.tensor_copy(
-            wt_dealt[:].rearrange("p a (t lines m) -> p a lines t m", t=PACK, m=4),
-            wt_raw[:].rearrange("p a (lines m t) -> p a lines t m", t=PACK, m=4),
+            wt_dealt[:].rearrange("p a (v e m) -> p a v m e", v=2, e=2),
+            wt_raw[:].rearrange("p a (m v e) -> p a v m e", v=2, e=2),
         )
         eye_codes = keep.tile([P, PACK * P], U32, name="eye_codes", align_bytes=64)
         eye_scales = keep.tile([P, PACK * P], U8, name="eye_scales", align_bytes=64)

import math
from contextlib import ExitStack

import concourse.mybir as mybir

K, L, N, T, J = 1024, 512, 512, 2048, 1024
FLOPS = 2 * N * J * (K + 3 * L)

F32 = mybir.dt.float32
BF16 = mybir.dt.bfloat16
I32 = mybir.dt.int32
U32 = mybir.dt.uint32
U16 = mybir.dt.uint16
U8 = mybir.dt.uint8
FP8X4 = mybir.dt.float8_e4m3fn_x4
FP4X4 = mybir.dt.float4_e2m1fn_x4
MULT = mybir.AluOpType.mult
ADD = mybir.AluOpType.add
SUB = mybir.AluOpType.subtract
EQUAL = mybir.AluOpType.is_equal
COPY = mybir.ActivationFunctionType.Copy

P = 128
QUADRANT = 32
PACK = 4
LIST_ROWS = 16
STRIP = 128
CHUNK = 256
HALF = 512
RUN = 4
EDGE = 64

MIDDLE = 3 * STRIP
LATE = 5 * STRIP
LAST = 7 * STRIP

VALUE_BANKS = (4, 5)
TURN_BANKS = ((6, 7), (0, 1))
TURN_BACK_BANK = 3
Y_BANKS = (0, 1, 2, 3, 6, 7, 0, 1)

FIRST_TIER, SECOND_TIER, PASS_0, PASS_1 = range(4)

Y_GROUPS = ((0, 2), (2, 3), (5, 1), (6, 2))


def woven(ap):
    return ap.rearrange("p (runs run t) -> p runs t run", run=RUN, t=PACK)


def by_rows(ap):
    return ap.rearrange("p t (runs run) -> p runs t run", run=RUN)


def tile_list_noneP_kernel(
    tc, xT, wgt, wt_words, wt_scales, c, wx_words, wx_scales, offs, out_0, out_1, out_2
):
    nc = tc.nc
    with ExitStack() as ctx:
        keep = ctx.enter_context(tc.tile_pool(name="keep", bufs=1))
        psum = ctx.enter_context(tc.psum_pool(name="psum", bufs=1))
        stage = ctx.enter_context(tc.tile_pool(name="stage", bufs=2))
        shared = ctx.enter_context(tc.tile_pool(name="shared", bufs=1))
        start_of = {"free": 0}

        def host(name, shape, dtype=F32, before=0, behind=0):
            start_of[name] = start_of["free"] + before
            start_of["free"] = start_of[name] + 4 * math.prod(shape[1:]) + behind
            return shared.tile(shape, dtype, name=name, offset=start_of[name], align_bytes=64)

        def tile_at(name, shape, dtype, place=None):
            if place is None:
                return keep.tile(shape, dtype, name=name, align_bytes=64)
            return shared.tile(shape, dtype, name=name, offset=start_of[place[0]] + place[1], align_bytes=64)

        offsets = keep.tile([P, J // LIST_ROWS], U16, name="offsets")
        nc.sync.dma_start(offsets[:], offs)

        stretches = J // P
        w_rows = keep.tile([P, P], F32, name="w_rows")
        nc.sync.dma_start(
            w_rows[:],
            wgt.rearrange("(g row) j -> g (row j)", row=LIST_ROWS)[:, : 2 * J].rearrange("g (cut m) -> g cut m", m=P),
        )

        woven_half = 2 * PACK * HALF
        c_sb = [
            host("c%d" % part, [P, PACK, CHUNK], before=woven_half if part == 2 else 0) for part in range(J // CHUNK)
        ]
        c_rows = c.rearrange("(p t) j -> p t j", t=PACK)

        def load_c(part):
            nc.sync.dma_start(c_sb[part][:], c_rows[:, :, part * CHUNK : (part + 1) * CHUNK])

        load_c(0)
        wx_raw = keep.tile([P, 2 * N], U8, name="wx_raw", align_bytes=64)
        nc.sync.dma_start(wx_raw[:].bitcast(I32), wx_words[0].bitcast(I32))

        chunk_codes = 4 * CHUNK
        scales_raw = host("scales_raw", [P, N // 4], I32, before=chunk_codes, behind=woven_half)
        nc.vector.memset(scales_raw[:], 0)

        square = keep.tile([P, P], F32, name="square")
        ones = keep.tile([P, P], F32, name="ones")
        nc.vector.memset(ones[:], 1.0)
        column = host("column", [P, P], behind=2 * PACK * P * PACK)
        nc.vector.tensor_tensor_scan(column[:], ones[:], ones[:], -1.0, MULT, ADD)
        in_quadrant = keep.tile([P, QUADRANT], F32, name="in_quadrant", align_bytes=64)
        nc.vector.transpose(in_quadrant[:], column[:, :QUADRANT])
        quadrant_start = keep.tile([P, 1], F32, name="quadrant_start")
        for p0 in range(0, P, QUADRANT):
            nc.vector.memset(quadrant_start[p0 : p0 + QUADRANT, :], float(p0))
        nc.vector.tensor_scalar(square[:], column[:], quadrant_start[:], in_quadrant[:, 0:1], SUB, EQUAL)

        eye = tile_at("eye", [P, PACK * P * PACK], BF16, ("column", 0))
        nc.vector.memset(eye[:].bitcast(I32), 0)
        for t in range(PACK):
            nc.vector.tensor_copy(eye[:, PACK * P * t + t : PACK * P * (t + 1) : PACK], square[:])

        planes = [host("plane%d" % u, [P, T]) for u in range(2 * PACK)]
        x_rows = xT.rearrange("(a p t) token -> a t p token", a=2, t=PACK)
        wt_raw = keep.tile([P, 2, N], I32, name="wt_raw", align_bytes=64)

        def load_plane(u):
            nc.sync.dma_start(planes[u][:], x_rows[u // PACK, u % PACK])

        def load_scales(q):
            p0 = QUADRANT * q
            nc.sync.dma_start(scales_raw[p0 : p0 + 4, :], wx_scales[0, 4 * q : 4 * q + 4, :].bitcast(I32))
            nc.sync.dma_start(scales_raw[p0 + 4 : p0 + 12, :], wt_scales[:, 4 * q : 4 * q + 4, :].bitcast(I32))

        load_plane(0)
        load_plane(1)
        load_c(1)
        load_scales(0)
        load_plane(2)
        load_scales(1)
        load_plane(3)
        load_scales(2)
        load_c(2)
        load_scales(3)
        load_plane(4)
        nc.sync.dma_start(wt_raw[:], wt_words.rearrange("a p n t -> p a (n t)").bitcast(I32))
        for u in range(5, 2 * PACK):
            load_plane(u)
        load_c(3)

        w_sb = keep.tile([P, J], F32, name="w_sb")
        w_turned = psum.tile([P, P], F32, name="w_turned", tag="bank2")
        nc.tensor.transpose(w_turned[:], w_rows[:], square[:])
        w_wide = keep.tile([P, J], F32, name="w_wide")
        nc.scalar.copy(
            w_wide[:].rearrange("m (z i again) -> m z i again", z=stretches, again=stretches),
            w_turned[:]
            .rearrange("m (i z) -> m z i", z=stretches)
            .unsqueeze(3)
            .to_broadcast([P, stretches, P // stretches, stretches]),
        )
        for h in range(2):
            w_back = psum.tile([P, HALF], F32, name="w_back", tag="bank%d" % h)
            for s in range(0, HALF, P):
                nc.tensor.transpose(w_back[:, s : s + P], w_wide[:, h * HALF + s : h * HALF + s + P], square[:])
            nc.scalar.copy(w_sb[:, h * HALF : (h + 1) * HALF], w_back[:])

        wx_dealt = keep.tile([P, 2 * N], U8, name="wx_dealt", align_bytes=64)
        nc.vector.tensor_copy(
            wx_dealt[:].rearrange("p (t lines m byte) -> p lines t m byte", t=PACK, m=8, byte=2),
            wx_raw[:].rearrange("p (lines m t byte) -> p lines t m byte", t=PACK, m=8, byte=2),
        )
        wt_dealt = keep.tile([P, 2, N], I32, name="wt_dealt", align_bytes=64)
        nc.vector.tensor_copy(
            wt_dealt[:].rearrange("p a (v e m) -> p a v m e", v=2, e=2),
            wt_raw[:].rearrange("p a (m v e) -> p a v m e", v=2, e=2),
        )
        eye_codes = keep.tile([P, PACK * P], U32, name="eye_codes", align_bytes=64)
        eye_scales = keep.tile([P, PACK * P], U8, name="eye_scales", align_bytes=64)
        nc.vector.quantize_mx(out=eye_codes[:].bitcast(FP8X4), scales=eye_scales[:], in_=eye[:])
        scales_dealt = keep.tile([P, N], U8, name="scales_dealt", align_bytes=64)
        nc.vector.tensor_copy(
            scales_dealt[:].rearrange("p (t lines m) -> p lines t m", t=PACK, m=16),
            scales_raw[:].bitcast(U8).rearrange("p (lines m t) -> p lines t m", t=PACK, m=16),
        )

        moving = ({}, {}, {}, {})

        def quantise(term, src, j0, width, place=None):
            codes = tile_at("codes%d_%d" % (term, j0), [P, width], U32, place)
            scales = tile_at("scales%d_%d" % (term, j0), [P, width], U8)
            nc.vector.quantize_mx(out=codes[:].bitcast(FP8X4), scales=scales[:], in_=src[:])
            for s in range(0, width, STRIP):
                moving[term][j0 + s] = (codes[:, s : s + STRIP], scales[:, s : s + STRIP])

        def gather(picked, base, u, j0, width):
            nc.vector.tensor_tensor(
                picked[:, u % PACK, j0 - base : j0 - base + width],
                planes[u][:].indirect(offsets[:, j0 // LIST_ROWS : (j0 + width) // LIST_ROWS]),
                w_sb[:, j0 : j0 + width],
                MULT,
            )

        def weave(copy, rounded, source, s, width):
            copy(woven(rounded[:]), by_rows(source[:, :, s : s + width]))
            return rounded

        def weave_c(part):
            return weave(nc.scalar.copy, tile_at("c_woven%d" % part, [P, PACK * CHUNK], BF16), c_sb[part], 0, CHUNK)

        def values_of(j):
            codes, scales = moving[FIRST_TIER][j]
            values = psum.tile([P, PACK, STRIP], F32, name="values", tag="bank%d" % VALUE_BANKS[j // STRIP % 2])
            for t in range(PACK):
                nc.tensor.matmul_mx(
                    out=values[:, t, :],
                    lhsT=eye_codes[:, t * P : (t + 1) * P].bitcast(FP8X4),
                    lhsT_scale=eye_scales[:, t * P : (t + 1) * P],
                    rhs=codes.bitcast(FP8X4),
                    rhs_scale=scales,
                    start=True,
                    stop=True,
                )
            return values

        def leftover_on_vector(part):
            left = tile_at("left%d" % part, [P, PACK * CHUNK], BF16)
            for s in range(0, CHUNK, STRIP):
                nc.vector.tensor_tensor(
                    woven(left[:, PACK * s : PACK * (s + STRIP)]),
                    by_rows(c_sb[part][:, :, s : s + STRIP]),
                    by_rows(values_of(part * CHUNK + s)[:]),
                    SUB,
                )
            return left

        def leftover_on_tensor(part, place=None):
            left = tile_at("left%d" % part, [P, PACK * CHUNK], BF16, place)
            turned_back = psum.tile([P, 2, 2, STRIP], F32, name="turned_back", tag="bank%d" % TURN_BACK_BANK)
            for b in range(CHUNK // STRIP):
                s = b * STRIP
                negated = stage.tile([P, PACK, STRIP], F32, name="negated")
                nc.scalar.activation(negated[:], values_of(part * CHUNK + s)[:], COPY, scale=-1.0)
                turned = psum.tile([P, PACK, P], F32, name="turned", tag="bank%d" % TURN_BANKS[part % 2][b])
                for addend, (source, col) in enumerate(((c_sb[part], s), (negated, 0))):
                    for t in range(PACK):
                        nc.tensor.matmul(
                            turned[:, t, :],
                            source[:, t, col : col + STRIP],
                            square[:],
                            start=(addend == 0 and t == 0),
                            stop=(addend == 1 and t == PACK - 1),
                            is_transpose=True,
                        )
                pairs = stage.tile([P, PACK * P], BF16, name="pairs")
                nc.scalar.copy(
                    pairs[:].rearrange("j (v p e) -> j v p e", v=2, e=2),
                    turned[:].rearrange("j (v e) p -> j v p e", v=2),
                )
                for v in range(2):
                    nc.tensor.transpose(turned_back[:, b, v, :], pairs[:].bitcast(F32)[:, v * P : (v + 1) * P], square[:])
            nc.scalar.copy(
                left[:].bitcast(F32).rearrange("p (b j v) -> p b j v", b=2, v=2),
                turned_back[:].rearrange("p b v j -> p b j v"),
            )
            return left

        sums = {}
        terms_left = {}

        def add_terms(b, terms):
            if FIRST_TIER in terms:
                sums[b] = psum.tile([P, PACK, STRIP], F32, name="sum", tag="bank%d" % Y_BANKS[b])
                terms_left[b] = len(moving)
            for term in terms:
                terms_left[b] = terms_left[b] - 1
                codes, scales = moving[term][b * STRIP]
                for t in range(PACK):
                    cols = slice(t * P, (t + 1) * P)
                    if term in (FIRST_TIER, SECOND_TIER):
                        weights = wx_dealt[:, 2 * t * P : 2 * (t + 1) * P].bitcast(FP4X4)
                        weight_scales = scales_dealt[:, cols]
                    else:
                        a = term - PASS_0
                        weights = wt_dealt[:, a, cols].bitcast(FP8X4)
                        weight_scales = scales_dealt[4 * (a + 1) : P, cols]
                    nc.tensor.matmul_mx(
                        out=sums[b][:, t, :],
                        lhsT=weights,
                        lhsT_scale=weight_scales,
                        rhs=codes.bitcast(FP8X4),
                        rhs_scale=scales,
                        start=(term == FIRST_TIER and t == 0),
                        stop=(terms_left[b] == 0 and t == PACK - 1),
                    )

        pass_0 = keep.tile([P, PACK, J], F32, name="pass_0")
        early = host("early", [P, PACK, MIDDLE])
        middle_row = keep.tile([P, PACK * (LATE - MIDDLE)], F32, name="middle", align_bytes=64)
        late_row = keep.tile([P, PACK * (J - LATE)], F32, name="late", align_bytes=64)
        middle = middle_row[:].rearrange("p (t j) -> p t j", t=PACK)
        late = late_row[:].rearrange("p (t j) -> p t j", t=PACK)
        gather(pass_0, 0, 0, 0, HALF)
        gather(pass_0, 0, 0, HALF, HALF)
        for u in range(1, PACK):
            gather(pass_0, 0, u, 0, J)
        for u in (4, 5):
            gather(early, 0, u, 0, MIDDLE)
            gather(middle, MIDDLE, u, MIDDLE, LATE - MIDDLE)
            gather(late, LATE, u, LATE, J - LATE)
        gather(early, 0, 6, 0, MIDDLE)

        quantise(FIRST_TIER, weave_c(0), 0, CHUNK)
        left_0 = leftover_on_tensor(0, ("c1", 0))
        quantise(FIRST_TIER, weave_c(1), CHUNK, CHUNK)
        quantise(SECOND_TIER, left_0, 0, CHUNK, ("scales_raw", EDGE - chunk_codes))
        left_1 = leftover_on_tensor(1, ("c2", EDGE))
        quantise(FIRST_TIER, weave_c(2), 2 * CHUNK, CHUNK)
        quantise(SECOND_TIER, left_1, CHUNK, CHUNK, ("plane4", 2 * chunk_codes))
        half_0 = tile_at("half_0", [P, PACK * HALF], BF16, ("scales_raw", EDGE))
        quantise(PASS_0, weave(nc.scalar.copy, half_0, pass_0, 0, HALF), 0, HALF, ("plane4", 0))
        left_2 = leftover_on_tensor(2)
        half_1 = tile_at("half_1", [P, PACK * HALF], BF16, ("c2", EDGE - woven_half))
        for s in (0, CHUNK):
            weave(nc.scalar.copy, half_1[:, PACK * s : PACK * (s + CHUNK)], pass_0, HALF + s, CHUNK)
        for b in range(HALF // STRIP):
            add_terms(b, (FIRST_TIER, SECOND_TIER, PASS_0))

        gather(early, 0, 7, 0, STRIP)
        gather(early, 0, 7, STRIP, CHUNK)
        strip_0 = weave(nc.scalar.copy, middle_row[:, 2 * CHUNK : 3 * CHUNK].bitcast(BF16), early, 0, STRIP)
        strips_1_2 = weave(nc.scalar.copy, late_row[:, 4 * CHUNK : 6 * CHUNK].bitcast(BF16), early, STRIP, CHUNK)
        quantise(PASS_1, strip_0, 0, STRIP)
        add_terms(0, (PASS_1,))
        gather(middle, MIDDLE, 6, MIDDLE, LATE - MIDDLE)
        gather(middle, MIDDLE, 7, MIDDLE, LATE - MIDDLE)
        quantise(PASS_1, strips_1_2, STRIP, CHUNK)
        add_terms(1, (PASS_1,))
        add_terms(2, (PASS_1,))

        c_woven_3 = weave_c(3)
        strips_3_4 = weave(nc.scalar.copy, tile_at("strips_3_4", [P, PACK * CHUNK], BF16), middle, 0, CHUNK)
        quantise(PASS_0, half_1, HALF, HALF, ("early", 0))
        quantise(SECOND_TIER, left_2, 2 * CHUNK, CHUNK, ("early", 2 * chunk_codes))
        gather(late, LATE, 6, LATE, J - LATE)
        quantise(PASS_1, strips_3_4, MIDDLE, CHUNK)
        add_terms(3, (PASS_1,))
        add_terms(4, (FIRST_TIER, PASS_0, SECOND_TIER, PASS_1))
        quantise(FIRST_TIER, c_woven_3, 3 * CHUNK, CHUNK)
        gather(late, LATE, 7, LATE, J - LATE)
        strips_5_6 = weave(nc.vector.tensor_copy, tile_at("strips_5_6", [P, PACK * CHUNK], BF16), late, 0, CHUNK)
        left_3 = leftover_on_vector(3)
        quantise(PASS_1, strips_5_6, LATE, CHUNK)
        add_terms(5, (FIRST_TIER, PASS_0, SECOND_TIER, PASS_1))
        strip_7 = weave(nc.vector.tensor_copy, tile_at("strip_7", [P, PACK * STRIP], BF16), late, LAST - LATE, STRIP)
        quantise(SECOND_TIER, left_3, 3 * CHUNK, CHUNK)
        quantise(PASS_1, strip_7, LAST, STRIP)

        y_codes = keep.tile([P, J], U32, name="y_codes", align_bytes=64)
        y_scales = keep.tile([P, J], U8, name="y_scales", align_bytes=64)
        y_rows = out_0.rearrange("(p t) j -> p t j", t=PACK)
        words_out = out_1[0].rearrange("p j t -> p (j t)").bitcast(I32)
        y_group = {}
        for b0, strips in Y_GROUPS:
            y_float = keep.tile([P, PACK, strips * STRIP], F32, name="y_float%d" % b0)
            y_woven = tile_at("y_woven%d" % b0, [P, PACK * strips * STRIP], BF16)
            for b in range(b0, b0 + strips):
                y_group[b] = (b0, strips, y_float, y_woven)

        def woven_part(b, strips):
            b0, y_woven = y_group[b][0], y_group[b][3]
            return y_woven[:, PACK * (b - b0) * STRIP : PACK * (b - b0 + strips) * STRIP]

        def copy_out(b):
            b0, strips, y_float = y_group[b][:3]
            nc.scalar.copy(y_float[:, :, (b - b0) * STRIP : (b - b0 + 1) * STRIP], sums[b][:])
            if b == b0 + strips - 1:
                nc.sync.dma_start(y_rows[:, :, b0 * STRIP : (b0 + strips) * STRIP], y_float[:])

        def round_from_bank(b):
            nc.scalar.copy(woven_part(b, 1).rearrange("p (j t) -> p j t", t=PACK), sums[b][:].rearrange("p t j -> p j t"))

        def round_from_copy(b, strips):
            b0, y_float = y_group[b][0], y_group[b][2]
            weave(nc.vector.tensor_copy, woven_part(b, strips), y_float, (b - b0) * STRIP, strips * STRIP)

        def quantise_y(b, strips):
            cols = slice(b * STRIP, (b + strips) * STRIP)
            nc.vector.quantize_mx(
                out=y_codes[:, cols].bitcast(FP8X4), scales=y_scales[:, cols], in_=woven_part(b, strips)
            )

        def store_words(b, strips):
            cols = slice(b * STRIP, (b + strips) * STRIP)
            nc.sync.dma_start(words_out[:, cols], y_codes[:, cols].bitcast(I32))

        first_late = LATE // STRIP
        for b in range(first_late):
            copy_out(b)
        for b in range(2, first_late):
            round_from_bank(b)
        add_terms(6, (FIRST_TIER, PASS_0, PASS_1, SECOND_TIER))
        add_terms(7, (FIRST_TIER, PASS_0, SECOND_TIER, PASS_1))
        quantise_y(2, 2)
        quantise_y(4, 1)
        store_words(2, 3)
        for b in range(first_late, J // STRIP):
            copy_out(b)
        round_from_copy(0, 2)
        round_from_copy(5, 1)
        quantise_y(0, 2)
        store_words(0, 2)
        round_from_copy(6, 1)
        quantise_y(5, 1)
        round_from_bank(7)
        quantise_y(6, 1)
        quantise_y(7, 1)
        store_words(5, 3)

        for q in range(4):
            queue = nc.scalar if q % 2 else nc.sync
            queue.dma_start(
                out_2[0, 4 * q : 4 * q + 4, :].bitcast(I32),
                y_scales[QUADRANT * q : QUADRANT * q + 4, :].bitcast(I32),
            )
